import numpy as np, ml_dtypes
CORES = [3,7,11,15,131,135,139,143]
N = 8
BF = ml_dtypes.bfloat16
W, R, P, STEPS, HOPS, SHIFT = 1024, 3072, 256, 3, 5, 3
def parts(rng):
    h = rng.integers(0, 256, (N, 8, 16, P)); w = rng.integers(0, 256, (N, 8, 16, 1)); t = rng.integers(700, 1300, (N, 8, 16, 1))
    m = rng.random((N, 8, W)) < rng.choice(np.array([0.1, 0.25, 0.5]), (N, 8, 1))
    return h, w, t, m, rng.integers(0, R, (N, 8, 16, W)), rng.integers(0, 256, (N, 8, 16, R))
def pack(h, w, t, m, o, r):
    m = m.astype(np.int32); m[..., 0] = 1
    b = lambda v, n: np.ascontiguousarray(v.reshape(N, 128, n)).astype(np.float32).astype(BF)
    i = lambda v, n: np.ascontiguousarray(v.reshape(N, 128, n)).astype(np.int32)
    return {"h0": b(h, P), "w": b(w, 1), "th": i(t, 1), "marks": m, "owner": i(o, W), "hdr": b(r, R)}
def far(rng, h, t, o, r, g, u=None):
    r[:, g] = rng.integers(128, 192, (N, 16, R))
    goal = np.where(np.arange(R) % 2 == 0, 4, 0) + rng.integers(0, 4, (N, R))
    r[:, g, 15] = 128 + ((goal - np.sum(r[:, g, :15], axis=1)) & 63)
    o[:, g] = (o[:, g] & -2) + (np.arange(16) & 1)[:, None]
    h[:, g] = rng.integers(0, 16, (N, 16, P))
    if u is not None: h[:, g, 0] = u >> 4; h[:, g, 1] = u & 15
    h[:, g, 15] = (-np.sum(h[:, g, :15], axis=1)) & 63
    t[:, g] = rng.integers(1300, 1751, (N, 16, 1))
def setup_inputs(rng):
    return pack(*parts(rng))
def setup_inputs_crowd(rng):
    h, w, t, m, o, r = parts(rng)
    w[:, 0::4] = 0; t[:, 0::4] = rng.integers(500, 1100, (N, 2, 16, 1))
    w[:, 1::4] = 0; w[:, 1::4, 0] = rng.integers(1, 4, (N, 2, 1)); h[:, 1::4, 0] = rng.integers(0, 3, (N, 2, P))
    w[:, 2::4] = 128 * rng.integers(0, 2, (N, 2, 16, 1))
    n = P // 16; lane = np.arange(P)
    far(rng, h, t, o, r, 4)
    start = rng.integers(0, n, (N, 16)); start[:, 0::4] = 0; start[:, 1::4] = n - 1; start[:, 3::4] = 1
    near = (lane >> 4) < start[:, lane & 15]
    h[:, 4] = np.where(near[:, None, :], rng.integers(128, 192, (N, 16, P)), h[:, 4])
    k = np.arange(256); found = np.unique((((k * k) >> 5) + k) & (W - 16), return_index=True)[1]
    order = np.argsort(rng.random((N, 16, len(found))), axis=-1)[..., :n]
    far(rng, h, t, o, r, 7, found[order].transpose(0, 2, 1).reshape(N, P))
    w[:, 7] = 0; w[:, 7, 0] = 16; w[:, 7, 1] = 1; m[:, 7] = True
    return pack(h, w, t, m, o, r)
def setup_inputs_ends(rng):
    h, w, t, m, o, r = parts(rng)
    k = np.arange(4096); tops = np.flatnonzero(((((k * k) >> 5) + k) & (W - 16)) == W - 16)
    u = rng.integers(0, 4096, (N, 6, P)); u[..., 0::32] = 0; u[..., 15::32] = rng.choice(tops, u[..., 15::32].shape)
    u[:, 4, 5::8] = rng.choice(tops, u[:, 4, 5::8].shape)
    w[:, :6] = 0; w[:, :6, 0] = 16; w[:, :6, 1] = 1; h[:, :6, 0] = u >> 4; h[:, :6, 1] = u & 15
    m[:, 0] = False; m[:, 1] = True; m[:, 2] = False; m[:, 2, W - 1] = True; m[:, 3] = True; m[:, 3, W - 1] = False; m[:, 4] = False; m[:, 4, 1] = True; m[:, 4, W - 16] = True
    t[:, 0:4:2] = rng.integers(0, 900, (N, 2, 16, 1)); t[:, 1] = rng.choice(np.array([0, 4096]), (N, 16, 1)); t[:, 5] = 0; t[:, 6] = 4096
    w[:, 7] = 255 - rng.integers(0, 16, (N, 16, 1)); h[:, 7] = 255 - rng.integers(0, 24, (N, 16, P)); w[0, 7] = 255; h[0, 7, :, 0::32] = 255
    return pack(h, w, t, m, o, r)
def setup_inputs_ties(rng):
    h, w, t, m, o, r = parts(rng)
    unit = rng.choice(np.array([8, 16]), (N, 8, 1, 1)); h = unit * (h // unit); r = unit * (r // unit)
    t = unit * (t // unit) + rng.choice(np.array([0, 0, 0, 1, -1]), t.shape)
    w[:, :2] = 0; m[:, :2, :16] = True; h[:, 1, :, :16] = 0; h[:, 1, 0, 1:16:2] = 1
    i = np.arange(16)
    for q in range(N):
        t[q, 0, :, 0] = np.sum(np.abs(r[q, 0][:, o[q, 0, :, 0]] - h[q, 0, :, 0:1]), axis=0)
        t[q, 1, :, 0] = np.sum(np.abs(r[q, 1][:, o[q, 1, i, i]] - h[q, 1, :, :16]), axis=0) + (i % 2 == 0)
    return pack(h, w, t, m, o, r)
def setup_inputs_alike(rng):
    h, w, t, m, o, r = parts(rng)
    o[:, ::2] = rng.choice(np.array([0, R - 1, R // 2, 3]), (N, 4, 16, W)); o[:, 1::4] = o[:, 1::4, :1].copy()
    r[..., 0] = 0; r[..., R - 1] = 255
    h[..., 0::7] = 0; h[..., 1::7] = 255; h[..., 3::7] = r[..., R // 2][..., None]
    t[:, 2] = 1
    t[:, 4] = 4080; t[:, 4, 1::4] = rng.choice(np.array([4081, 4096]), (N, 4, 1)); o[:, 4, 1::4] = R - 1; o[:, 4, 12] = 3
    t[:, 6] = 0; o[:, 6, 1::4] = R // 2; o[:, 6, 0] = 3
    return pack(h, w, t, m, o, r)
def setup_inputs_spread(rng):
    h, w, t, m, o, r = parts(rng)
    h = (np.exp2(8 * rng.random((N, 8, 1, P))) * rng.random((N, 8, 16, P))).astype(np.int64)
    r = (np.exp2(8 * rng.random((N, 8, 1, R))) * rng.random((N, 8, 16, R))).astype(np.int64)
    w = np.minimum(np.exp2(8 * rng.random((N, 8, 16, 1))).astype(np.int64), 255)
    t = np.minimum(np.exp2(12 * rng.random((N, 8, 16, 1))).astype(np.int64), 4096)
    m = rng.random((N, 8, W)) < np.exp2(-8 * rng.random((N, 8, 1)))
    o = np.minimum((R * rng.random((N, 8, 16, W)) ** 3).astype(np.int64), R - 1)
    return pack(h, w, t, m, o, r)
def check_inputs(d):
    bad = []
    for k, hi in (("h0", 255), ("w", 255), ("th", 4096), ("marks", 1), ("owner", R - 1), ("hdr", 255)):
        v = np.asarray(d[k]).astype(np.float32)
        if not np.all((v >= 0) & (v <= hi) & (v == np.floor(v))): bad.append("range of " + k)
    if not np.all(np.asarray(d["marks"])[..., 0] == 1): bad.append("address 0 is a boundary")
    return bad
def reference(h0, w, th, marks, owner, hdr):
    h = h0.astype(np.float32).astype(np.int64).reshape(N, 8, 16, P); wt = w.astype(np.float32).astype(np.int64).reshape(N, 8, 16, 1)
    t = th.astype(np.int64).reshape(N, 8, 1, 16); m = marks > 0; o = owner.astype(np.int64).reshape(N, 8, 16, W)
    r = hdr.astype(np.float32).astype(np.int32).reshape(N, 8, 16, R)
    port = np.arange(P) & 15; slot = np.arange(16)
    for step in range(STEPS):
        u = np.add.reduce(wt * h, axis=2) & 4095
        x = ((((u * u) >> 5) + u) & (W - 16)) + port
        top = np.maximum.accumulate(np.where(m, np.arange(W), 0), axis=2)
        a = np.take_along_axis(top, x, 2); b = np.take_along_axis(top, (a - 1) & (W - 1), 2)
        ra = np.take_along_axis(o, a[:, :, None, :], 3); rb = np.take_along_axis(o, b[:, :, None, :], 3)
        new = []
        for q in range(N):
            ids = np.ascontiguousarray(ra[q].transpose(0, 2, 1)).reshape(8, 1, P * 16)
            v = np.take_along_axis(r[q], ids, 2).reshape(8, 16, P, 16)
            d = np.add.reduce(np.abs(v - h[q][..., None]), axis=1)
            n = np.where(d < t[q], slot, (d >> 2) & 15)
            e = np.zeros((8, P), np.int64) + port
            for hop in range(HOPS):
                e = np.take_along_axis(n, e[..., None], 2)[..., 0]
            done = np.take_along_axis(n, e[..., None], 2)[..., 0] == e
            ve = np.take_along_axis(v, e[:, None, :, None], 3)[..., 0]
            new.append(np.where(done[:, None, :], (h[q] + ve) >> 1, np.abs(h[q] - ve)))
            col = np.where(slot[None, :, None] == e[:, None, :], rb[q], ra[q])
            for g in range(8):
                lanes = np.flatnonzero(~done[g])
                xs, first = np.unique(x[q, g, lanes], return_index=True)
                o[q, g][:, xs] = col[g][:, lanes[first]]
                m[q, g, xs] = True
        h = np.roll(np.stack(new), SHIFT, axis=0)
    return {"yh": h.reshape(N, 128, P).astype(np.float32).astype(BF), "yo": o.reshape(N, 128, W).astype(np.float32), "ym": m.astype(np.float32)}

@@ -1,0 +1,479 @@
+import numpy as np
+from concourse.mybir import AluOpType as A, ActivationFunctionType as AF
+
+N, P, W, R, STEPS, SHIFT = 8, 256, 1024, 3072, 3, 3
+PARTS = [(0, 128), (128, 256)]
+CHUNKS = [[[("v", 64)], [("v", 32), ("a", 32)]], [[("v", 64)], [("v", 32), ("a", 32)]]]
+HXD = [5, 5]
+SENDS = [(0, 128), (128, 256)]
+MAG = 12582912.0
+INIT = 2000.0
+
+SCRATCH = {}
+for _n, _w in (("oc", W), ("D0", W + P), ("D1", W + P), ("YO", W + P), ("YM", W + P), ("ST", W), ("sF", 1), ("s16", 1), ("s4", 1),
+               ("thF", 1), ("s4t", 1), ("s8F", 1), ("sm1", 1), ("Lb0", 16), ("Lb", 16), ("dm0", 16), ("dmp", 16), ("z16", 16),
+               ("NE", P), ("RST", P), ("KI", P), ("K1", P), ("xf", 16), ("dx0", 16), ("dx", 16), ("SF", P), ("a1", P), ("Ac", P),
+               ("Rr", P), ("b1", P), ("B0", P), ("wr", P), ("tw", P), ("col", P), ("F1", 1), ("F2", 1), ("fx", P), ("gx", P),
+               ("t2", 16), ("bd", 16), ("val", P), ("sc", P), ("ls", 16), ("kl", 16), ("kd", 16)):
+    SCRATCH[_n] = ("sbuf", [128, _w], "float32")
+for _n, _w in (("hdS", R), ("mkB", W), ("wS", 1), ("ones", 128), ("BO1", 128), ("BO", 128), ("G8", 128), ("Q", 144), ("WQ", 144),
+               ("ID", 128), ("ID2", 128), ("nI", 128), ("B16", 128), ("nB16", 128), ("BSn", 128), ("BSp", 128), ("M0", P),
+               ("hx", 16 * P), ("D", 16 * P), ("AB", 16 * P), ("V", 16 * P), ("E", P), ("E5", P), ("X", P), ("XF", P), ("Dg", P),
+               ("Ba", P), ("bm", P), ("hb0", P), ("hb1", P), ("hb2", P), ("hb3", P), ("hn0", P), ("hn1", P), ("hn2", P)):
+    SCRATCH[_n] = ("sbuf", [128, _w], "bfloat16")
+for _n, _w in (("ow", W), ("mkI", W), ("thI", 1), ("pI", 1), ("sI", 1), ("s8I", 1), ("tauI", 1), ("mI", P), ("mJ", P), ("rI", P),
+               ("uI", 16), ("uM", 16), ("u32", 16), ("pr", 16), ("rw", 16), ("md", P), ("q4", P), ("aI", P)):
+    SCRATCH[_n] = ("sbuf", [128, _w], "int32")
+for _n, _w in (("jl", 16), ("jh", 16), ("PA", P), ("xl", 16), ("OL", 16), ("xs", 16)):
+    SCRATCH[_n] = ("sbuf", [128, _w], "uint16")
+PSUM = ["pd0", "pd1", "pn0", "pn1", "pr0", "pr1", "pL", "pY"]
+for _n in PSUM:
+    SCRATCH[_n] = ("psum", [128, 512], "float32")
+QSEM = {"dve": "qv", "pe": "qt", "act": "qa", "g": "qg"}
+DMAS = ["lh", "lw", "lt", "lm", "lo0", "lo1", "lr", "syo", "sym"] + ["syh%d" % k for k in range(len(SENDS))]
+SEMAPHORES = list(QSEM.values()) + DMAS + ["%s%d%d" % (k, t, h) for k in ("ar", "sn") for t in range(STEPS) for h in range(len(SENDS))]
+EST = {"c": 1.0, "g": 1.6, "s": 3.6, "op": 10.0, "wake": 80.0, "own": 40.0, "net": 2000.0, "rem": 600.0, "dma": 2200.0, "win": 150.0}
+SC = [dict(), dict(c=.85, g=.9, s=1.5, wake=50), dict(c=1.2, g=2.4, s=6.5), dict(g=1.1, s=5.0, wake=150, own=80, rem=900, net=2500),
+      dict(g=2.1, s=2.0, wake=30, own=20, rem=400, net=1500, dma=1800)]
+TRIES = 2000
+CACHE = {}
+
+
+def build(T, rank, core, topo):
+    ops, ctx = [], {"h": 0, "t": 0}
+
+    def node(q, work, reads, writes, emit, **kw):
+        nm = writes[0][0] if writes else kw.get("sem", "x")
+        ops.append(dict(q=q, work=work, reads=reads, writes=writes, emit=emit, tag=nm + str(ctx["h"]), t=ctx["t"], **kw))
+
+    def rg(name, a=0, b=None, st=1):
+        return (name, a, SCRATCH[name][1][1] if b is None else b, st)
+
+    def ap(r):
+        n, a, b, st = r
+        return T[n][:, a:b] if st == 1 else T[n][:, a:b:st]
+
+    width = lambda r: (r[2] - r[1] + r[3] - 1) // r[3]
+    ind = lambda win, off: ap(win).indirect(ap(off))
+    isp = lambda r: r[0] in PSUM
+    two = lambda r: SCRATCH[r[0]][2] in ("bfloat16", "uint16")
+    cyc = lambda n, k=1.0: ("c", max(64, n * k))
+    val = lambda s: ap(s) if isinstance(s, tuple) else s
+    regs = lambda *s: [x for x in s if isinstance(x, tuple)]
+    def copy(o, i):
+        node("dve", [cyc(width(o), 0.5 if two(o) and two(i) else 1)], [i], [o], lambda e: [e.tensor_copy(ap(o), ap(i))])
+    def tt(o, x, y, op):
+        node("dve", [cyc(width(o), 1 if isp(x) or isp(y) else 2)], [x, y], [o], lambda e: [e.tensor_tensor(ap(o), ap(x), ap(y), op)])
+    def ts(o, x, s1, s2, op0, op1=None):
+        def emit(e):
+            if op1 is None:
+                return [e.tensor_scalar(ap(o), ap(x), val(s1), None, op0)]
+            return [e.tensor_scalar(ap(o), ap(x), val(s1), val(s2), op0, op1)]
+        node("dve", [cyc(width(o), 0.5 if two(o) and two(x) else 1)], [x] + regs(s1, s2), [o], emit)
+    def fill(o, c):
+        node("dve", [cyc(width(o), 0.5 if two(o) else 1)], [], [o], lambda e: [e.memset(ap(o), c)])
+    def scan(o, x, y, init, op0, op1):
+        node("dve", [cyc(width(o))], [x, y], [o], lambda e: [e.tensor_tensor_scan(ap(o), ap(x), ap(y), init, op0, op1)])
+    def g_tt(o, win, off, y, op):
+        node("dve", [("k", 55), ("g", width(o))], [win, off, y], [o], lambda e: [e.tensor_tensor(ap(o), ind(win, off), ap(y), op)])
+    def g_ts(o, win, off, s1, s2, op0, op1):
+        node("dve", [("k", 55), ("g", width(o))], [win, off], [o], lambda e: [e.tensor_scalar(ap(o), ind(win, off), s1, s2, op0, op1)])
+    def scat(win, off, i):
+        node("dve", [("k", 55), ("s", width(i))], [i, off], [win], lambda e: [e.tensor_copy(ind(win, off), ap(i))])
+    def scat_add(win, off, i, c):
+        node("dve", [("k", 55), ("s", width(i))], [i, off], [win], lambda e: [e.tensor_scalar(ind(win, off), ap(i), 1.0, c, A.mult, A.add)])
+    def act(o, i, f, bias=0.0, scale=1.0):
+        node("act", [cyc(width(o))], [i] + regs(bias, scale), [o], lambda e: [e.activation(ap(o), ap(i), f, bias=val(bias), scale=val(scale))])
+    def g_act(o, win, off):
+        node("act", [("k", 70), ("g", width(o))], [win, off], [o], lambda e: [e.activation(ap(o), ind(win, off), AF.Copy)])
+    def mm(o, pairs):
+        def emit(e):
+            n = len(pairs)
+            return [e.matmul(ap(o), ap(l), ap(r), j == 0, j == n - 1) for j, (l, r) in enumerate(pairs)]
+        node("pe", [cyc(width(r)) for _, r in pairs], sorted(set([l for l, _ in pairs] + [r for _, r in pairs])), [o], emit)
+    sel = lambda q, s: rg(q, 15 - s, 143 - s)
+    def dma(q, sem, reads, writes, out, in_, ns):
+        node(q, [("k", 60)], reads, writes, lambda e: [e.dma_start(out(), in_())], sem=sem, count=16, lat=[("dma", 1), ("k", ns)])
+
+    dma("sp", "lm", [], [rg("mkI")], lambda: T.mkI[0:8, :], lambda: T.marks[:], 0)
+    dma("act", "lw", [], [rg("wS")], lambda: T.wS[:], lambda: T.w[:], 0)
+    dma("sp", "lo0", [], [rg("ow", 0, 512)], lambda: T.ow[:, 0:512], lambda: T.owner[:, 0:512], 1200)
+    dma("act", "lh", [], [rg("hb0")], lambda: T.hb0[:], lambda: T.h0[:], 400)
+    dma("sp", "lo1", [], [rg("ow", 512, W)], lambda: T.ow[:, 512:W], lambda: T.owner[:, 512:W], 2400)
+    dma("act", "lt", [], [rg("thI")], lambda: T.thI[:], lambda: T.th[:], 1200)
+    dma("sp", "lr", [], [rg("hdS")], lambda: T.hdS[:], lambda: T.hdr[:], 6000)
+
+    fill(rg("ones"), 1.0)
+    gn = lambda n, reads, o, f: node("g", [("k", 150), ("c", 2 * n)], reads, [o], lambda e: [f(e)])
+    gn(128, [rg("ones")], rg("G8"), lambda e: e.affine_select(T.G8[0:8, :], T.ones[0:8, :], [[-1, 8], [0, 16]], A.is_equal, 0.0, 0, 1))
+    gn(128, [rg("ones")], rg("BO1"), lambda e: e.affine_select(T.BO1[:], T.ones[:], [[-16, 8], [0, 16]], A.is_ge, 0.0, 0, 1))
+    gn(128, [rg("BO1")], rg("BO"), lambda e: e.affine_select(T.BO[:], T.BO1[:], [[16, 8], [0, 16]], A.is_ge, 0.0, 15, -1))
+    gn(128, [rg("ones")], rg("ID"), lambda e: e.affine_select(T.ID[:], T.ones[:], [[-1, 128]], A.is_equal, 0.0, 0, 1))
+    gn(1, [], rg("pI"), lambda e: e.iota(T.pI[:], [[1, 1]], 0, 1))
+    gn(256, [], rg("mI"), lambda e: e.iota(T.mI[:], [[1, 256]], 128, -1))
+    gn(16, [], rg("Lb0"), lambda e: e.iota(T.Lb0[:], [[256, 16]], 0, 0, allow_small_or_imprecise_dtypes=True))
+    gn(16, [], rg("dm0"), lambda e: e.iota(T.dm0[:], [[16, 16]], W, 0, allow_small_or_imprecise_dtypes=True))
+    gn(64, [], rg("rI", 0, 64), lambda e: e.iota(T.rI[:, 0:64], [[0, 8], [1, 8]], 0, 0))
+    gn(128, [], rg("rI", 64, 192), lambda e: e.iota(T.rI[:, 64:192], [[0, 8], [1, 16]], 0, 0))
+
+    fill(rg("Q"), 0.0)
+    copy(rg("Q", 15, 143, 16), rg("BO", 0, 128, 16))
+    ts(rg("WQ"), rg("Q"), rg("wS"), None, A.mult)
+    ts(rg("sI"), rg("pI"), 15, None, A.bitwise_and)
+    copy(rg("sF"), rg("sI"))
+    node("dve", [cyc(1024)], [rg("mkI")], [rg("mkB")], lambda e: [e.tensor_copy(T.mkB[0:8, :], T.mkI[0:8, :])])
+    for b in range(2):
+        node("pe", [cyc(512)], [rg("G8"), rg("mkB", 512 * b, 512 * b + 512)], [rg("pd%d" % b)],
+             lambda e, b=b: [e.matmul(T["pd%d" % b][:], T.G8[0:8, :], T.mkB[0:8, 512 * b:512 * b + 512], True, True)])
+    B = lambda n, b: rg(n, 512 * b, 512 * b + 512)
+    for b in range(2):
+        act(B("D0", b), rg("pd%d" % b), AF.Identity, 1.0, 1.0 / 8192 - 1.0)
+        ts(B("oc", b), B("ow", b), -1536.0, None, A.add)
+        tt(B("D1", b), rg("pd%d" % b), B("oc", b), A.mult)
+    ts(rg("s4"), rg("sF"), 4.0, None, A.mult)
+    ts(rg("s16"), rg("sF"), 16.0, None, A.mult)
+    copy(rg("thF"), rg("thI"))
+    ts(rg("tauI"), rg("thI"), 60, None, A.bitwise_and)
+    tt(rg("s4t"), rg("s4"), rg("tauI"), A.subtract)
+    ts(rg("ID2"), rg("ID"), 2.0, None, A.mult)
+    ts(rg("nI"), rg("ID"), -1.0, None, A.mult)
+    ts(rg("B16"), rg("BO"), 1.0 / 16, None, A.mult)
+    ts(rg("nB16"), rg("BO"), -16.0, None, A.mult)
+    ts(rg("sm1"), rg("sF"), -1.0 / 16, None, A.mult)
+    ts(rg("BSn"), rg("BO"), rg("sm1"), None, A.mult)
+    ts(rg("BSp"), rg("BO"), rg("s16"), None, A.mult)
+    ts(rg("mJ"), rg("mI"), 15, None, A.bitwise_and)
+    ts(rg("M0"), rg("mJ"), 0.0, None, A.is_equal)
+    ts(rg("Lb"), rg("Lb0"), rg("s16"), None, A.add)
+    ts(rg("dmp"), rg("dm0"), rg("sF"), None, A.add)
+    fill(rg("z16"), 0.0)
+    ts(rg("jl"), rg("z16"), rg("sF"), None, A.add)
+    ts(rg("s8I"), rg("sI"), 7, None, A.bitwise_and)
+    copy(rg("s8F"), rg("s8I"))
+    ts(rg("jh"), rg("z16"), rg("s8F"), None, A.add)
+    fill(rg("NE"), 10000.0)
+    ts(rg("RST", 0, 192), rg("rI", 0, 192), 0.0, 1000000.0, A.is_equal, A.mult)
+    fill(rg("KI"), 1.0 / 8192)
+    fill(rg("K1"), 1.0)
+    act(rg("YO", 0, W), rg("oc"), AF.Identity, 1536.0)
+
+    for t in range(STEPS):
+        ctx["t"] = t
+        hb = "hb%d" % t
+        for h, (p0, p1) in enumerate(PARTS):
+            ctx["h"] = h
+            for s in range(16):
+                o, i = rg("hx", 16 * p0 + s, 16 * p1, 16), rg(hb, p0, p1)
+                if s < HXD[h]:
+                    copy(o, i)
+                else:
+                    act(o, i, AF.Copy)
+        ctx["h"] = 0
+        mm(rg("pL", 0, 16), [(sel("WQ", r), rg(hb, r, P, 16)) for r in range(16)])
+        copy(rg("uI"), rg("pL", 0, 16))
+        ts(rg("uM"), rg("uI"), 4095, None, A.bitwise_and)
+        ts(rg("u32"), rg("uM"), 32.0, None, A.add)
+        tt(rg("pr"), rg("uM"), rg("u32"), A.mult)
+        ts(rg("rw"), rg("pr"), 5, 1008, A.arith_shift_right, A.bitwise_and)
+        ts(rg("xl"), rg("rw"), rg("sF"), None, A.add)
+        scan(rg("ST"), rg("D0", 0, W), rg("D1", 0, W), INIT, A.mult, A.add)
+        for h, (p0, p1) in enumerate(PARTS):
+            ctx["h"] = h
+            g_ts(rg("PA", p0, p1), rg("ST"), rg("xl", p0 // 16, p1 // 16), MAG + 1536.0, MAG, A.add, A.subtract)
+        ctx["h"] = 0
+        ts(rg("xf"), rg("rw"), rg("sF"), None, A.add)
+        tt(rg("dx0"), rg("dmp"), rg("xf"), A.subtract)
+        ts(rg("dx"), rg("dx0"), 1.0 / 16, None, A.mult)
+        for h in range(2):
+            ctx["h"] = h
+            base = lambda c: c * 8 if c < 8 else 64 + (c - 8) * 16
+            def emit_ne(e, cs=range(max(1, 8 * h), 8 * h + 8), base=base):
+                return [e.activation(T.NE[:, base(c):base(c) + c], T.xf[:, 0:c], AF.Abs, bias=T.xf[:, c:c + 1], scale=-1.0) for c in cs]
+            node("act", [cyc(16)] * 8, [rg("xf")], [rg("NE", 0, 64) if h == 0 else rg("NE", 64, 192)], emit_ne)
+        ctx["h"] = 0
+        g_act(rg("SF"), rg("ST"), rg("xl"))
+        ts(rg("F1"), rg("ST", W - 1, W), MAG, MAG, A.add, A.subtract)
+        ts(rg("F2"), rg("F1"), -INIT, None, A.add)
+        act(rg("a1"), rg("SF"), AF.Identity, MAG)
+        act(rg("pY", 256, 512), rg("a1"), AF.Identity, -MAG)
+        act(rg("Ac"), rg("a1"), AF.Identity, -MAG)
+        tt(rg("Rr"), rg("SF"), rg("pY", 256, 512), A.subtract)
+        act(rg("b1"), rg("Rr"), AF.Identity, MAG, 8192.0)
+        act(rg("B0"), rg("b1"), AF.Identity, -MAG)
+        act(rg("wr"), rg("B0"), AF.Relu, -1999.0)
+        act(rg("tw"), rg("wr"), AF.Identity, 0.0, rg("F2"))
+        tt(rg("pY", 0, 256), rg("B0"), rg("pY", 256, 512), A.subtract)
+        tt(rg("pY", 0, 256), rg("pY", 0, 256), rg("tw"), A.add)
+        for h, (p0, p1) in enumerate(PARTS):
+            ctx["h"] = h
+            HL, c0, c1 = p1 - p0, p0 // 16, p1 // 16
+            H = lambda name: rg(name, p0, p1)
+            L = lambda name: rg(name, c0, c1)
+            pd, pn, pq = "pd%d" % h, "pn%d" % h, "pr%d" % h
+            m1 = p0
+            for ch in CHUNKS[h]:
+                l0 = m1
+                for mode, k in ch:
+                    m0, m1 = m1, m1 + k
+                    cols = (16 * m0, 16 * m1)
+                    if mode == "v":
+                        g_tt(rg("D", *cols), rg("hdS"), rg("PA", m0, m1), rg("hx", *cols), A.subtract)
+                        act(rg("AB", *cols), rg("D", *cols), AF.Abs)
+                    else:
+                        ps = rg(pq, 0, 16 * k)
+                        g_act(rg("V", *cols), rg("hdS"), rg("PA", m0, m1))
+                        mm(ps, [(rg("nI"), rg("hx", *cols)), (rg("ID"), rg("V", *cols))])
+                        act(rg("AB", *cols), ps, AF.Abs)
+                        act(rg("D", *cols), ps, AF.Copy)
+                mm(rg(pd, l0 - p0, m1 - p0), [(sel("Q", s), rg("AB", 16 * l0 + s, 16 * m1, 16)) for s in range(16)])
+            d, n4 = rg(pd, 0, HL), rg(pn, 0, HL)
+            ts(H("md"), d, rg("thF"), None, A.max)
+            ts(n4, d, rg("thF"), rg("s4t"), A.is_lt, A.mult)
+            ts(H("q4"), H("md"), 60, None, A.bitwise_and)
+            tt(n4, n4, H("q4"), A.add)
+            X, rv = H("X"), rg(pq, 0, HL)
+            tt(X, n4, H("M0"), A.mult)
+            ts(H("fx"), n4, rg("s4"), 16.0, A.is_equal, A.mult)
+            act(H("gx"), H("fx"), AF.Identity, rg("sF"))
+            for k in range(5):
+                mm(rv, [(rg("BO"), X)])
+                E = H("E") if k < 4 else H("E5")
+                ts(E, rv, rg("s4"), None, A.is_equal)
+                if k < 4:
+                    tt(X, n4, E, A.mult)
+            OL, pl = L("OL"), rg("pL", 16 + c0, 16 + c1)
+            tt(H("XF"), H("gx"), H("E5"), A.mult)
+            mm(pl, [(sel("Q", r), rg("XF", p0 + r, p1, 16)) for r in range(16)])
+            ts(L("bd"), pl, 16.0, 16.0, A.is_ge, A.mult)
+            tt(L("t2"), pl, rg("Lb", 0, c1 - c0), A.add)
+            tt(OL, L("t2"), L("bd"), A.subtract)
+            mu, hv, zB, am = rg(pq, HL, 2 * HL), rg(pd, HL, 2 * HL), rg(pq, 2 * HL, 3 * HL), rg(pn, 2 * HL, 3 * HL)
+            mm(mu, [(rg("B16"), H("XF")), (rg("BSn"), H("E5"))])
+            g_act(H("Dg"), rg("D", 16 * p0, 16 * p1), OL)
+            mm(hv, [(rg("ID2"), H(hb)), (rg("ID"), H("Dg"))])
+            act(H("Ba"), H("Dg"), AF.Abs)
+            mm(zB, [(rg("nB16"), H("XF")), (rg("BSp"), H("E5")), (rg("ID"), H("Ba"))])
+            act(H("bm"), zB, AF.Relu)
+            ts(H("aI"), hv, 0.5, -0.25, A.mult, A.add)
+            tt(am, H("aI"), mu, A.mult)
+            tt(H("hn%d" % t), am, H("bm"), A.add)
+            for k, (s0, s1) in enumerate(SENDS):
+                if not p0 < s1 <= p1:
+                    continue
+                dst = T.cores[(rank + SHIFT) % N]
+                hn, nx = rg("hn%d" % t, s0, s1), rg("hb%d" % (t + 1), s0, s1)
+                def send(e, hn=hn, nx=nx, t=t, k=k, dst=dst):
+                    rid, pid = topo.addr(dst, core)
+                    e.remote_dma(ap(nx), ap(hn), T.sem["ar%d%d" % (t, k)], T.sem["sn%d%d" % (t, k)], pid, rid, topo.mask(core, dst))
+                    return []
+                ne = len(topo.engines(core, dst))
+                node("g", [("rem", 1)], [hn], [], send, sem="sn%d%d" % (t, k), count=ne, lat=[("net", 0.5)])
+                node("net", [], [], [nx], None, sem="ar%d%d" % (t, k), count=ne, lat=[("net", 1)], after=len(ops) - 1)
+            nr, q0, q1 = (8, 0, 64) if h == 0 else (16, 64, 192)
+            if h == 0:
+                g_tt(rg("val", q0, q1), rg("bd", 0, 8), rg("jh", 0, 4), rg("NE", q0, q1), A.add)
+            else:
+                g_tt(rg("val", q0, q1), rg("bd"), rg("jl", 0, 8), rg("NE", q0, q1), A.add)
+            scan(rg("sc", q0, q1), rg("RST", q0, q1), rg("val", q0, q1), 1000000.0, A.add, A.min)
+            ts(L("ls"), rg("sc", q0 + nr - 1, q1, nr), 0.5, 16.0, A.is_le, A.mult)
+            tt(L("kl"), L("bd"), L("ls"), A.max)
+            tt(L("kd"), L("kl"), L("dx"), A.mult)
+            tt(L("xs"), L("kd"), L("xf"), A.add)
+            tt(rg("pY", 256 + p0, 256 + p1), rg("pY", p0, p1), H("E5"), A.mult)
+            tt(H("col"), rg("pY", 256 + p0, 256 + p1), H("Ac"), A.add)
+            if t < STEPS - 1:
+                scat(rg("D0"), L("xs"), H("KI"))
+                scat(rg("D1"), L("xs"), H("col"))
+                if t == STEPS - 2 and h == 1:
+                    act(rg("YM", 0, W), rg("D0", 0, W), AF.Sign, 1.0, -1.0)
+            scat_add(rg("YO"), L("xs"), H("col"), 1536.0)
+            if t == STEPS - 1:
+                scat(rg("YM"), L("xs"), H("K1"))
+    ctx["h"] = 2
+    dma("sp", "syo", [rg("YO", 0, W)], [], lambda: T.yo[:], lambda: T.YO[:, 0:W], 3000)
+    dma("act", "sym", [rg("YM", 0, W)], [], lambda: T.ym[:], lambda: T.YM[0:128:16, 0:W], 0)
+    for k, (s0, s1) in enumerate(SENDS):
+        dma("sp", "syh%d" % k, [rg("hb3", s0, s1)], [], lambda s0=s0, s1=s1: T.yh[:, s0:s1], lambda s0=s0, s1=s1: T.hb3[:, s0:s1], 200)
+    return ops
+
+
+def meet(a, b):
+    if a[1] >= b[2] or b[1] >= a[2]:
+        return False
+    if a[3] == b[3] and a[3] > 1:
+        return (a[1] - b[1]) % a[3] == 0
+    return True
+
+
+def depend(ops):
+    hist, deps = {}, []
+    for i, o in enumerate(ops):
+        d = {}
+        for w, regs in ((0, o["reads"]), (1, o["writes"])):
+            for r in regs:
+                for (j, pw, pr) in hist.get(r[0], []):
+                    same = ops[j]["q"] == o["q"] and o["q"] != "net"
+                    bank = r[0] in PSUM and not same
+                    if bank or ((w or pw) and meet(r, pr)):
+                        d[j] = d.get(j, False) or not same or bool(pw)
+        if "after" in o:
+            d[o["after"]] = True
+        d.pop(i, None)
+        deps.append(d)
+        for w, regs in ((0, o["reads"]), (1, o["writes"])):
+            for r in regs:
+                lst = hist.setdefault(r[0], [])
+                if w and r[0] not in PSUM and r[3] == 1:
+                    lst[:] = [x for x in lst if not (r[1] <= x[2][1] and x[2][2] <= r[2])]
+                lst.append((i, w, r))
+    return deps
+
+
+def price(work, est):
+    return sum(n if k == "k" else n * est[k] + (est["op"] if k == "c" else 0.0) for k, n in work)
+
+
+def schedule(ops, deps, est, bias):
+    n = len(ops)
+    cost = [price(o["work"], est) for o in ops]
+    lat = [price(o.get("lat", []), est) for o in ops]
+    succ = [[] for _ in range(n)]
+    for i in range(n):
+        for j in deps[i]:
+            succ[j].append(i)
+    prio = [0.0] * n
+    for i in range(n - 1, -1, -1):
+        prio[i] = cost[i] + lat[i] + max([prio[k] + (est["wake"] if ops[k]["q"] != ops[i]["q"] else est["own"]) for k in succ[i]] + [0.0])
+    rank = [prio[i] + bias.get(ops[i]["tag"], 0.0) for i in range(n)]
+    left = [len(deps[i]) for i in range(n)]
+    free, fin, order, begin = {}, [0.0] * n, [], [0.0] * n
+    ready = {}
+
+    def enter(i):
+        q = ops[i]["q"]
+        s = 0.0
+        for j, hard in deps[i].items():
+            if ops[j]["q"] != q:
+                s = max(s, fin[j] + est["wake"])
+            elif hard:
+                s = max(s, fin[j] + est["own"])
+        begin[i] = s
+        ready.setdefault(q, []).append(i)
+    for i in range(n):
+        if left[i] == 0:
+            enter(i)
+    while True:
+        bq, bs = None, 1e18
+        for q, lst in ready.items():
+            if lst:
+                s = max(free.get(q, 0.0), min(begin[i] for i in lst))
+                if s < bs:
+                    bq, bs = q, s
+        if bq is None:
+            break
+        c = [i for i in ready[bq] if begin[i] <= bs + est["win"]]
+        i = max(c, key=lambda k: rank[k] - max(0.0, begin[k] - bs))
+        ready[bq].remove(i)
+        order.append(i)
+        end = max(free.get(bq, 0.0), begin[i]) + cost[i]
+        if bq != "net":
+            free[bq] = end
+        fin[i] = end + lat[i]
+        for k in succ[i]:
+            left[k] -= 1
+            if left[k] == 0:
+                enter(k)
+    return order
+
+
+def tune(ops, deps):
+    n = len(ops)
+    q = [o["q"] for o in ops]
+    pars = []
+    for sc in SC:
+        e = dict(EST)
+        e.update(sc)
+        pars.append((e, [price(o["work"], e) for o in ops], [price(o.get("lat", []), e) for o in ops]))
+    dl = [[(j, q[j] == q[i]) for j, hard in deps[i].items() if hard or q[j] != q[i] or q[i] == "net"] for i in range(n)]
+
+    def span(order, e, cost, lat):
+        fin, free = [0.0] * n, {}
+        for i in order:
+            f = free.get(q[i], 0.0) if q[i] != "net" else 0.0
+            t = f
+            for j, same in dl[i]:
+                x = fin[j]
+                if x > f - 1e-9 or same:
+                    t = max(t, x + (e["own"] if same else e["wake"]))
+            free[q[i]] = t + cost[i]
+            fin[i] = t + cost[i] + lat[i]
+        return max(fin)
+    best, order = {}, schedule(ops, deps, EST, {})
+    base = [span(order, *p) for p in pars]
+    score = float(len(pars))
+    tags = sorted(set(o["tag"] for o in ops if o["q"] in QSEM))
+    rnd = np.random.RandomState(0)
+    for _ in range(TRIES):
+        b = dict(best)
+        for _ in range([1, 1, 2, 3, 5][int(rnd.randint(5))]):
+            k = tags[int(rnd.randint(len(tags)))]
+            if rnd.rand() < 0.2:
+                b.pop(k, None)
+            else:
+                b[k] = float(round(b.get(k, 0.0) + 3000.0 * rnd.randn()))
+        o = schedule(ops, deps, EST, b)
+        v = sum(span(o, *p) / x for p, x in zip(pars, base))
+        if v < score - 1e-7:
+            best, order, score = b, o, v
+    return order
+
+
+def rank_program(g, core, T, topo):
+    rank = T.rank_of(core)
+    if rank is None:
+        return
+    ops = build(T, rank, core, topo)
+    if "order" not in CACHE:
+        CACHE["deps"] = depend(ops)
+        CACHE["order"] = tune(ops, CACHE["deps"])
+    deps, order = CACHE["deps"], CACHE["order"]
+    eng = {"dve": g.vector, "pe": g.tensor, "act": g.scalar, "g": g, "sp": g.sync}
+    total, known, done = {}, {q: {} for q in eng}, {}
+    for i in order:
+        o = ops[i]
+        q = o["q"]
+        if q == "net":
+            total[o["sem"]] = o["count"]
+            done[i] = (o["sem"], o["count"], {})
+            continue
+        need, clocks = {}, {}
+        for j, hard in deps[i].items():
+            if ops[j]["q"] == q and not hard:
+                continue
+            s, v, ck = done[j]
+            if v > need.get(s, 0):
+                need[s], clocks[s] = v, ck
+        kn = known[q]
+        todo = [(s, v) for s, v in need.items() if kn.get(s, 0) < v]
+        for s, v in todo:
+            if not any(s2 != s and clocks[s2].get(s, 0) >= v for s2, _ in todo):
+                eng[q].wait_ge(T.sem[s], v)
+        for s, v in todo:
+            kn[s] = max(kn.get(s, 0), v)
+            for s3, v3 in clocks[s].items():
+                kn[s3] = max(kn.get(s3, 0), v3)
+        ins = o["emit"](eng[q])
+        if "sem" in o:
+            for x in ins:
+                x.then_inc(T.sem[o["sem"]], o["count"])
+            total[o["sem"]] = o["count"]
+            done[i] = (o["sem"], o["count"], dict(kn))
+        else:
+            s = QSEM[q]
+            for x in ins:
+                x.then_inc(T.sem[s], 1)
+            total[s] = total.get(s, 0) + len(ins)
+            done[i] = (s, total[s], dict(kn))
+    for s, v in total.items():
+        if known["g"].get(s, 0) < v:
+            g.wait_ge(T.sem[s], v)

@@ -2,40 +2,43 @@ import numpy as np
 from concourse.mybir import AluOpType as A, ActivationFunctionType as AF
 
 N, P, W, R, STEPS, SHIFT = 8, 256, 1024, 3072, 3, 3
-PARTS = [(0, 128), (128, 256)]
-CHUNKS = [[[("v", 64)], [("v", 32), ("a", 32)]], [[("v", 64)], [("v", 32), ("a", 32)]]]
-HXD = [5, 5]
-SENDS = [(0, 128), (128, 256)]
+HL = 128
+CHUNKS = [[("v", 64), ("a", 32), ("a", 32)], [("v", 64), ("v", 32), ("a", 32)]]
+HXD = [2, 0]
+HXG = [0, 6]
 MAG = 12582912.0
 INIT = 2000.0
 
-SCRATCH = {}
-for _n, _w in (("oc", W), ("D0", W + P), ("D1", W + P), ("YO", W + P), ("YM", W + P), ("ST", W), ("sF", 1), ("s16", 1), ("s4", 1),
-               ("thF", 1), ("s4t", 1), ("s8F", 1), ("sm1", 1), ("Lb0", 16), ("Lb", 16), ("dm0", 16), ("dmp", 16), ("z16", 16),
-               ("NE", P), ("RST", P), ("KI", P), ("K1", P), ("xf", 16), ("dx0", 16), ("dx", 16), ("SF", P), ("a1", P), ("Ac", P),
-               ("Rr", P), ("b1", P), ("B0", P), ("wr", P), ("tw", P), ("col", P), ("F1", 1), ("F2", 1), ("fx", P), ("gx", P),
-               ("t2", 16), ("bd", 16), ("val", P), ("sc", P), ("ls", 16), ("kl", 16), ("kd", 16)):
+COLF = ["sF", "s4", "s128", "thH", "thL", "taN", "s8F", "aF", "pb", "s8x", "F1", "F2", "F3"]
+SCRATCH = {"cf": ("sbuf", [128, len(COLF)], "float32")}
+for _n, _w in (("oc", W), ("D0", W + P), ("D1", W + P), ("YO", W + P), ("YM", W + P), ("ST", W), ("thT", HL), ("s4T", HL),
+               ("pk0", 8), ("pS0", 16), ("pS", 16), ("LB0", 24), ("LB1", 24), ("LC0", 32), ("LC1", 32), ("dm0", 16), ("dm1", 16),
+               ("dmp", 16), ("z16", 16), ("NE", P), ("RST", P), ("xf", 16), ("SF", P), ("a1", P), ("Rr", P), ("b1", P), ("B0", P),
+               ("tw", P), ("BA", P), ("t5", P), ("col0", P), ("col1", P), ("col2", P),
+               ("bd", 16), ("val", P), ("sc", P), ("ls", 16), ("kl", 16), ("kd", 16)):
     SCRATCH[_n] = ("sbuf", [128, _w], "float32")
 for _n, _w in (("hdS", R), ("mkB", W), ("wS", 1), ("ones", 128), ("BO1", 128), ("BO", 128), ("G8", 128), ("Q", 144), ("WQ", 144),
-               ("ID", 128), ("ID2", 128), ("nI", 128), ("B16", 128), ("nB16", 128), ("BSn", 128), ("BSp", 128), ("M0", P),
-               ("hx", 16 * P), ("D", 16 * P), ("AB", 16 * P), ("V", 16 * P), ("E", P), ("E5", P), ("X", P), ("XF", P), ("Dg", P),
-               ("Ba", P), ("bm", P), ("hb0", P), ("hb1", P), ("hb2", P), ("hb3", P), ("hn0", P), ("hn1", P), ("hn2", P)):
+               ("ID", 128), ("ID2", 128), ("nI", 128), ("TH", 128), ("TL", 128), ("TN", 128), ("RE", 40), ("RF", 40), ("M0", 128),
+               ("hp", P), ("hx", 16 * P), ("D", 32 * P), ("AB", 16 * P), ("V", 16 * P), ("E", P), ("E5", P), ("X", P), ("XF", P),
+               ("Dg", P), ("Bg", P), ("hm", P), ("hb0", 2 * P), ("hb1", 2 * P), ("hb2", 2 * P), ("hb3", P), ("hn0", P), ("hn1", P),
+               ("hn2", P)):
     SCRATCH[_n] = ("sbuf", [128, _w], "bfloat16")
-for _n, _w in (("ow", W), ("mkI", W), ("thI", 1), ("pI", 1), ("sI", 1), ("s8I", 1), ("tauI", 1), ("mI", P), ("mJ", P), ("rI", P),
-               ("uI", 16), ("uM", 16), ("u32", 16), ("pr", 16), ("rw", 16), ("md", P), ("q4", P), ("aI", P)):
+for _n, _w in (("ow", W), ("mkI", W), ("thI", 1), ("thX", 1), ("thY", 1), ("pI", 1), ("sI", 1), ("s8I", 1), ("aI1", 1), ("tauI", 1),
+               ("mI", 128), ("mJ", 128), ("rI", P), ("uI", 16), ("uM", 16), ("u32", 16), ("pr", 16), ("rw", 16), ("vI", 16),
+               ("vM", 16), ("v32", 16), ("vr", 16), ("vw", 16), ("md", P), ("q4", P), ("aI", P)):
     SCRATCH[_n] = ("sbuf", [128, _w], "int32")
-for _n, _w in (("jl", 16), ("jh", 16), ("PA", P), ("xl", 16), ("OL", 16), ("xs", 16)):
+for _n, _w in (("jl", 16), ("jh", 16), ("prm", 8), ("PA", P), ("xl", 16), ("xj", 16), ("OL", 64), ("xs0", 16), ("xs1", 16), ("xs2", 16)):
     SCRATCH[_n] = ("sbuf", [128, _w], "uint16")
 PSUM = ["pd0", "pd1", "pn0", "pn1", "pr0", "pr1", "pL", "pY"]
 for _n in PSUM:
     SCRATCH[_n] = ("psum", [128, 512], "float32")
 QSEM = {"dve": "qv", "pe": "qt", "act": "qa", "g": "qg"}
-DMAS = ["lh", "lw", "lt", "lm", "lo0", "lo1", "lr", "syo", "sym"] + ["syh%d" % k for k in range(len(SENDS))]
-SEMAPHORES = list(QSEM.values()) + DMAS + ["%s%d%d" % (k, t, h) for k in ("ar", "sn") for t in range(STEPS) for h in range(len(SENDS))]
-EST = {"c": 1.0, "g": 1.6, "s": 3.6, "op": 10.0, "wake": 80.0, "own": 40.0, "net": 2000.0, "rem": 600.0, "dma": 2200.0, "win": 150.0}
+DMAS = ["lh", "lw", "lt", "lm", "lo0", "lo1", "lr", "syo", "sym", "syh0", "syh1"]
+SEMAPHORES = list(QSEM.values()) + DMAS + ["%s%d%d" % (k, t, h) for k in ("ar", "sn") for t in range(STEPS) for h in range(2)]
+EST = {"c": 1.0, "g": 1.6, "s": 3.6, "op": 10.0, "wake": 80.0, "own": 40.0, "net": 2000.0, "rem": 600.0, "dma": 2200.0, "win": 100.0}
 SC = [dict(), dict(c=.85, g=.9, s=1.5, wake=50), dict(c=1.2, g=2.4, s=6.5), dict(g=1.1, s=5.0, wake=150, own=80, rem=900, net=2500),
       dict(g=2.1, s=2.0, wake=30, own=20, rem=400, net=1500, dma=1800)]
-TRIES = 2000
+TRIES = 3000
 CACHE = {}
 
 
@@ -47,6 +50,8 @@ def build(T, rank, core, topo):
         ops.append(dict(q=q, work=work, reads=reads, writes=writes, emit=emit, tag=nm + str(ctx["h"]), t=ctx["t"], **kw))
 
     def rg(name, a=0, b=None, st=1):
+        if name in COLF:
+            return ("cf", COLF.index(name), COLF.index(name) + 1, 1)
         return (name, a, SCRATCH[name][1][1] if b is None else b, st)
 
     def ap(r):
@@ -74,23 +79,28 @@ def build(T, rank, core, topo):
         node("dve", [cyc(width(o), 0.5 if two(o) else 1)], [], [o], lambda e: [e.memset(ap(o), c)])
     def scan(o, x, y, init, op0, op1):
         node("dve", [cyc(width(o))], [x, y], [o], lambda e: [e.tensor_tensor_scan(ap(o), ap(x), ap(y), init, op0, op1)])
+    def g_copy(o, win, off):
+        node("dve", [("k", 55), ("g", width(o))], [win, off], [o], lambda e: [e.tensor_copy(ap(o), ind(win, off))])
     def g_tt(o, win, off, y, op):
         node("dve", [("k", 55), ("g", width(o))], [win, off, y], [o], lambda e: [e.tensor_tensor(ap(o), ind(win, off), ap(y), op)])
     def g_ts(o, win, off, s1, s2, op0, op1):
         node("dve", [("k", 55), ("g", width(o))], [win, off], [o], lambda e: [e.tensor_scalar(ap(o), ind(win, off), s1, s2, op0, op1)])
     def scat(win, off, i):
         node("dve", [("k", 55), ("s", width(i))], [i, off], [win], lambda e: [e.tensor_copy(ind(win, off), ap(i))])
-    def scat_add(win, off, i, c):
-        node("dve", [("k", 55), ("s", width(i))], [i, off], [win], lambda e: [e.tensor_scalar(ind(win, off), ap(i), 1.0, c, A.mult, A.add)])
+    def scat_add(win, off, i, c, k=1.0):
+        node("dve", [("k", 55), ("s", width(i))], [i, off], [win], lambda e: [e.tensor_scalar(ind(win, off), ap(i), k, c, A.mult, A.add)])
     def act(o, i, f, bias=0.0, scale=1.0):
         node("act", [cyc(width(o))], [i] + regs(bias, scale), [o], lambda e: [e.activation(ap(o), ap(i), f, bias=val(bias), scale=val(scale))])
-    def g_act(o, win, off):
-        node("act", [("k", 70), ("g", width(o))], [win, off], [o], lambda e: [e.activation(ap(o), ind(win, off), AF.Copy)])
+    def g_act(o, win, off, f=AF.Copy):
+        node("act", [("k", 70), ("g", width(o))], [win, off], [o], lambda e: [e.activation(ap(o), ind(win, off), f)])
     def mm(o, pairs):
         def emit(e):
             n = len(pairs)
             return [e.matmul(ap(o), ap(l), ap(r), j == 0, j == n - 1) for j, (l, r) in enumerate(pairs)]
         node("pe", [cyc(width(r)) for _, r in pairs], sorted(set([l for l, _ in pairs] + [r for _, r in pairs])), [o], emit)
+    def mms(triples):
+        node("pe", [cyc(width(r)) for _, _, r in triples], sorted(set([l for _, l, _ in triples] + [r for _, _, r in triples])),
+             [o for o, _, _ in triples], lambda e: [e.matmul(ap(o), ap(l), ap(r), True, True) for o, l, r in triples])
     sel = lambda q, s: rg(q, 15 - s, 143 - s)
     def dma(q, sem, reads, writes, out, in_, ns):
         node(q, [("k", 60)], reads, writes, lambda e: [e.dma_start(out(), in_())], sem=sem, count=16, lat=[("dma", 1), ("k", ns)])
@@ -98,7 +108,7 @@ def build(T, rank, core, topo):
     dma("sp", "lm", [], [rg("mkI")], lambda: T.mkI[0:8, :], lambda: T.marks[:], 0)
     dma("act", "lw", [], [rg("wS")], lambda: T.wS[:], lambda: T.w[:], 0)
     dma("sp", "lo0", [], [rg("ow", 0, 512)], lambda: T.ow[:, 0:512], lambda: T.owner[:, 0:512], 1200)
-    dma("act", "lh", [], [rg("hb0")], lambda: T.hb0[:], lambda: T.h0[:], 400)
+    dma("act", "lh", [], [rg("hb0", 0, P)], lambda: T.hb0[:, 0:P], lambda: T.h0[:], 400)
     dma("sp", "lo1", [], [rg("ow", 512, W)], lambda: T.ow[:, 512:W], lambda: T.owner[:, 512:W], 2400)
     dma("act", "lt", [], [rg("thI")], lambda: T.thI[:], lambda: T.th[:], 1200)
     dma("sp", "lr", [], [rg("hdS")], lambda: T.hdS[:], lambda: T.hdr[:], 6000)
@@ -108,11 +118,23 @@ def build(T, rank, core, topo):
     gn(128, [rg("ones")], rg("G8"), lambda e: e.affine_select(T.G8[0:8, :], T.ones[0:8, :], [[-1, 8], [0, 16]], A.is_equal, 0.0, 0, 1))
     gn(128, [rg("ones")], rg("BO1"), lambda e: e.affine_select(T.BO1[:], T.ones[:], [[-16, 8], [0, 16]], A.is_ge, 0.0, 0, 1))
     gn(128, [rg("BO1")], rg("BO"), lambda e: e.affine_select(T.BO[:], T.BO1[:], [[16, 8], [0, 16]], A.is_ge, 0.0, 15, -1))
-    gn(128, [rg("ones")], rg("ID"), lambda e: e.affine_select(T.ID[:], T.ones[:], [[-1, 128]], A.is_equal, 0.0, 0, 1))
     gn(1, [], rg("pI"), lambda e: e.iota(T.pI[:], [[1, 1]], 0, 1))
-    gn(256, [], rg("mI"), lambda e: e.iota(T.mI[:], [[1, 256]], 128, -1))
-    gn(16, [], rg("Lb0"), lambda e: e.iota(T.Lb0[:], [[256, 16]], 0, 0, allow_small_or_imprecise_dtypes=True))
-    gn(16, [], rg("dm0"), lambda e: e.iota(T.dm0[:], [[16, 16]], W, 0, allow_small_or_imprecise_dtypes=True))
+    fl = dict(allow_small_or_imprecise_dtypes=True)
+    gn(16, [], rg("pS0"), lambda e: e.iota(T.pS0[:], [[0, 2], [2, 8]], 0, 0, **fl))
+    gn(8, [], rg("pk0"), lambda e: e.iota(T.pk0[:], [[2, 8]], 0, 0, **fl))
+    gn(128, [rg("ones")], rg("ID"), lambda e: e.affine_select(T.ID[:], T.ones[:], [[-1, 128]], A.is_equal, 0.0, 0, 1))
+    gn(128, [], rg("mI"), lambda e: e.iota(T.mI[:], [[1, 128]], 128, -1))
+    for h in range(2):
+        lb = "LB%d" % h
+        gn(16, [], rg(lb, 0, 16), lambda e, lb=lb: e.iota(T[lb][:, 0:16], [[-2048, 2], [16, 8]], 2048, 0, **fl))
+        gn(8, [], rg(lb, 16, 24), lambda e, lb=lb, h=h: e.iota(T[lb][:, 16:24], [[16, 8]], 256 + 128 * h, 0, **fl))
+    gn(16, [], rg("dm0"), lambda e: e.iota(T.dm0[:], [[16, 16]], W, 0, **fl))
+    def zero(o):
+        gn(width(o), [], o, lambda e: e.iota(ap(o), [[0, width(o)]], 0, 0, **fl))
+    for k in range(2):
+        zero(rg("hb%d" % k, P, 2 * P))
+        zero(rg("D", 4096 * k + 2048, 4096 * k + 4096))
+    zero(rg("hb2", P, 2 * P))
     gn(64, [], rg("rI", 0, 64), lambda e: e.iota(T.rI[:, 0:64], [[0, 8], [1, 8]], 0, 0))
     gn(128, [], rg("rI", 64, 192), lambda e: e.iota(T.rI[:, 64:192], [[0, 8], [1, 16]], 0, 0))
 
@@ -121,6 +143,14 @@ def build(T, rank, core, topo):
     ts(rg("WQ"), rg("Q"), rg("wS"), None, A.mult)
     ts(rg("sI"), rg("pI"), 15, None, A.bitwise_and)
     copy(rg("sF"), rg("sI"))
+    ts(rg("s8I"), rg("sI"), 7, None, A.bitwise_and)
+    copy(rg("s8F"), rg("s8I"))
+    ts(rg("aI1"), rg("sI"), 3, None, A.arith_shift_right)
+    copy(rg("aF"), rg("aI1"))
+    ts(rg("s8x"), rg("s8F"), 16.0, None, A.mult)
+    tt(rg("pb"), rg("s8x"), rg("aF"), A.add)
+    ts(rg("prm"), rg("pk0"), rg("pb"), None, A.add)
+    ts(rg("pS"), rg("pS0"), rg("aF"), None, A.add)
     node("dve", [cyc(1024)], [rg("mkI")], [rg("mkB")], lambda e: [e.tensor_copy(T.mkB[0:8, :], T.mkI[0:8, :])])
     for b in range(2):
         node("pe", [cyc(512)], [rg("G8"), rg("mkB", 512 * b, 512 * b + 512)], [rg("pd%d" % b)],
@@ -131,59 +161,79 @@ def build(T, rank, core, topo):
         ts(B("oc", b), B("ow", b), -1536.0, None, A.add)
         tt(B("D1", b), rg("pd%d" % b), B("oc", b), A.mult)
     ts(rg("s4"), rg("sF"), 4.0, None, A.mult)
-    ts(rg("s16"), rg("sF"), 16.0, None, A.mult)
-    copy(rg("thF"), rg("thI"))
-    ts(rg("tauI"), rg("thI"), 60, None, A.bitwise_and)
-    tt(rg("s4t"), rg("s4"), rg("tauI"), A.subtract)
-    ts(rg("ID2"), rg("ID"), 2.0, None, A.mult)
-    ts(rg("nI"), rg("ID"), -1.0, None, A.mult)
-    ts(rg("B16"), rg("BO"), 1.0 / 16, None, A.mult)
-    ts(rg("nB16"), rg("BO"), -16.0, None, A.mult)
-    ts(rg("sm1"), rg("sF"), -1.0 / 16, None, A.mult)
-    ts(rg("BSn"), rg("BO"), rg("sm1"), None, A.mult)
-    ts(rg("BSp"), rg("BO"), rg("s16"), None, A.mult)
+    ts(rg("s128"), rg("sF"), 128.0, None, A.mult)
     ts(rg("mJ"), rg("mI"), 15, None, A.bitwise_and)
     ts(rg("M0"), rg("mJ"), 0.0, None, A.is_equal)
-    ts(rg("Lb"), rg("Lb0"), rg("s16"), None, A.add)
-    ts(rg("dmp"), rg("dm0"), rg("sF"), None, A.add)
+    ts(rg("thX"), rg("thI"), 8128, None, A.bitwise_and)
+    ts(rg("thY"), rg("thI"), 63, None, A.bitwise_and)
+    ts(rg("tauI"), rg("thI"), 60, None, A.bitwise_and)
+    copy(rg("thH"), rg("thX"))
+    copy(rg("thL"), rg("thY"))
+    ts(rg("taN"), rg("tauI"), -1.0, None, A.mult)
+    ts(rg("TH"), rg("BO"), rg("thH"), None, A.mult)
+    ts(rg("TL"), rg("BO"), rg("thL"), None, A.mult)
+    ts(rg("TN"), rg("BO"), rg("taN"), None, A.mult)
+    mm(rg("pn0", 0, HL), [(rg("M0"), rg("TH")), (rg("M0"), rg("TL"))])
+    mm(rg("pn0", HL, 2 * HL), [(rg("M0"), rg("TN"))])
+    copy(rg("thT"), rg("pn0", 0, HL))
+    ts(rg("s4T"), rg("pn0", HL, 2 * HL), rg("s4"), None, A.add)
+    ts(rg("ID2"), rg("ID"), 2.0, None, A.mult)
+    ts(rg("nI"), rg("ID"), -1.0, None, A.mult)
+    dc = rg("BO", 0, 128, 16)
+    fill(rg("RE"), 0.0)
+    fill(rg("RF"), 0.0)
+    for k in (0, 1, 3):
+        ts(rg("RE", 8 * k, 8 * k + 8), dc, rg("sF"), None, A.mult)
+    for k, c in ((0, -2048.0), (1, 2048.0), (2, -256.0), (4, 16.0)):
+        ts(rg("RF", 8 * k, 8 * k + 8), dc, c, None, A.mult)
+    for h in range(2):
+        ts(rg("LC%d" % h, 0, 16), rg("LB%d" % h, 0, 16), rg("s128"), None, A.add)
+        ts(rg("LC%d" % h, 16, 24), rg("LB%d" % h, 16, 24), rg("sF"), None, A.add)
+        fill(rg("LC%d" % h, 24, 32), 0.0)
+    ts(rg("dm1"), rg("dm0"), rg("sF"), None, A.add)
+    ts(rg("dmp"), rg("dm1"), 1.0 / 16, None, A.mult)
     fill(rg("z16"), 0.0)
     ts(rg("jl"), rg("z16"), rg("sF"), None, A.add)
-    ts(rg("s8I"), rg("sI"), 7, None, A.bitwise_and)
-    copy(rg("s8F"), rg("s8I"))
     ts(rg("jh"), rg("z16"), rg("s8F"), None, A.add)
     fill(rg("NE"), 10000.0)
     ts(rg("RST", 0, 192), rg("rI", 0, 192), 0.0, 1000000.0, A.is_equal, A.mult)
-    fill(rg("KI"), 1.0 / 8192)
-    fill(rg("K1"), 1.0)
     act(rg("YO", 0, W), rg("oc"), AF.Identity, 1536.0)
 
     for t in range(STEPS):
         ctx["t"] = t
         hb = "hb%d" % t
-        for h, (p0, p1) in enumerate(PARTS):
+        for h in range(2):
             ctx["h"] = h
+            p0, p1 = HL * h, HL * h + HL
+            g_act(rg("hp", p0, p1), rg(hb, p0, p1), rg("prm"))
             for s in range(16):
-                o, i = rg("hx", 16 * p0 + s, 16 * p1, 16), rg(hb, p0, p1)
+                o, i = rg("hx", 16 * p0 + s, 16 * p1, 16), rg("hp", p0, p1)
                 if s < HXD[h]:
                     copy(o, i)
+                elif s >= 16 - HXG[h]:
+                    gn(HL, [i], o, lambda e, o=o, i=i: e.affine_select(ap(o), ap(i), [[0, HL]], A.is_ge, 0.0, 0, 0))
                 else:
                     act(o, i, AF.Copy)
+            mm(rg("pL", 8 * h, 8 * h + 8), [(sel("WQ", q), rg(hb, p0 + 16 * (q % 8) + q // 8, p0 + 16 * (q % 8) + 16, 2)) for q in range(16)])
         ctx["h"] = 0
-        mm(rg("pL", 0, 16), [(sel("WQ", r), rg(hb, r, P, 16)) for r in range(16)])
         copy(rg("uI"), rg("pL", 0, 16))
         ts(rg("uM"), rg("uI"), 4095, None, A.bitwise_and)
         ts(rg("u32"), rg("uM"), 32.0, None, A.add)
         tt(rg("pr"), rg("uM"), rg("u32"), A.mult)
         ts(rg("rw"), rg("pr"), 5, 1008, A.arith_shift_right, A.bitwise_and)
-        ts(rg("xl"), rg("rw"), rg("sF"), None, A.add)
+        tt(rg("xl"), rg("rw"), rg("pS"), A.add)
+        mm(rg("pL", 16, 32), [(sel("WQ", r), rg(hb, r, P, 16)) for r in range(16)])
+        copy(rg("vI"), rg("pL", 16, 32))
+        ts(rg("vM"), rg("vI"), 4095, None, A.bitwise_and)
+        ts(rg("v32"), rg("vM"), 32.0, None, A.add)
+        tt(rg("vr"), rg("vM"), rg("v32"), A.mult)
+        ts(rg("vw"), rg("vr"), 5, 1008, A.arith_shift_right, A.bitwise_and)
+        ts(rg("xj"), rg("vw"), rg("sF"), None, A.add)
+        ts(rg("xf"), rg("vw"), rg("sF"), None, A.add)
         scan(rg("ST"), rg("D0", 0, W), rg("D1", 0, W), INIT, A.mult, A.add)
-        for h, (p0, p1) in enumerate(PARTS):
+        for h in range(2):
             ctx["h"] = h
-            g_ts(rg("PA", p0, p1), rg("ST"), rg("xl", p0 // 16, p1 // 16), MAG + 1536.0, MAG, A.add, A.subtract)
-        ctx["h"] = 0
-        ts(rg("xf"), rg("rw"), rg("sF"), None, A.add)
-        tt(rg("dx0"), rg("dmp"), rg("xf"), A.subtract)
-        ts(rg("dx"), rg("dx0"), 1.0 / 16, None, A.mult)
+            g_ts(rg("PA", HL * h, HL * h + HL), rg("ST"), rg("xl", 8 * h, 8 * h + 8), MAG + 1536.0, MAG, A.add, A.subtract)
         for h in range(2):
             ctx["h"] = h
             base = lambda c: c * 8 if c < 8 else 64 + (c - 8) * 16
@@ -191,84 +241,78 @@ def build(T, rank, core, topo):
                 return [e.activation(T.NE[:, base(c):base(c) + c], T.xf[:, 0:c], AF.Abs, bias=T.xf[:, c:c + 1], scale=-1.0) for c in cs]
             node("act", [cyc(16)] * 8, [rg("xf")], [rg("NE", 0, 64) if h == 0 else rg("NE", 64, 192)], emit_ne)
         ctx["h"] = 0
-        g_act(rg("SF"), rg("ST"), rg("xl"))
+        pA, pB = rg("pY", 256, 512), rg("pY", 0, 256)
+        g_act(rg("SF"), rg("ST"), rg("xj"))
         ts(rg("F1"), rg("ST", W - 1, W), MAG, MAG, A.add, A.subtract)
-        ts(rg("F2"), rg("F1"), -INIT, None, A.add)
+        ts(rg("F2"), rg("F1"), -1.0, INIT, A.mult, A.add)
+        ts(rg("F3"), rg("F2"), -1999.0, None, A.mult)
         act(rg("a1"), rg("SF"), AF.Identity, MAG)
-        act(rg("pY", 256, 512), rg("a1"), AF.Identity, -MAG)
-        act(rg("Ac"), rg("a1"), AF.Identity, -MAG)
-        tt(rg("Rr"), rg("SF"), rg("pY", 256, 512), A.subtract)
+        act(pA, rg("a1"), AF.Identity, -MAG)
+        tt(rg("Rr"), rg("SF"), pA, A.subtract)
         act(rg("b1"), rg("Rr"), AF.Identity, MAG, 8192.0)
         act(rg("B0"), rg("b1"), AF.Identity, -MAG)
-        act(rg("wr"), rg("B0"), AF.Relu, -1999.0)
-        act(rg("tw"), rg("wr"), AF.Identity, 0.0, rg("F2"))
-        tt(rg("pY", 0, 256), rg("B0"), rg("pY", 256, 512), A.subtract)
-        tt(rg("pY", 0, 256), rg("pY", 0, 256), rg("tw"), A.add)
-        for h, (p0, p1) in enumerate(PARTS):
+        act(rg("tw"), rg("B0"), AF.Relu, rg("F3"), rg("F2"))
+        tt(pB, rg("B0"), pA, A.subtract)
+        tt(rg("BA"), pB, rg("tw"), A.subtract)
+        for h in range(2):
             ctx["h"] = h
-            HL, c0, c1 = p1 - p0, p0 // 16, p1 // 16
+            p0, p1, c0, c1 = HL * h, HL * h + HL, 8 * h, 8 * h + 8
             H = lambda name: rg(name, p0, p1)
             L = lambda name: rg(name, c0, c1)
             pd, pn, pq = "pd%d" % h, "pn%d" % h, "pr%d" % h
             m1 = p0
-            for ch in CHUNKS[h]:
-                l0 = m1
-                for mode, k in ch:
-                    m0, m1 = m1, m1 + k
-                    cols = (16 * m0, 16 * m1)
-                    if mode == "v":
-                        g_tt(rg("D", *cols), rg("hdS"), rg("PA", m0, m1), rg("hx", *cols), A.subtract)
-                        act(rg("AB", *cols), rg("D", *cols), AF.Abs)
-                    else:
-                        ps = rg(pq, 0, 16 * k)
-                        g_act(rg("V", *cols), rg("hdS"), rg("PA", m0, m1))
-                        mm(ps, [(rg("nI"), rg("hx", *cols)), (rg("ID"), rg("V", *cols))])
-                        act(rg("AB", *cols), ps, AF.Abs)
-                        act(rg("D", *cols), ps, AF.Copy)
-                mm(rg(pd, l0 - p0, m1 - p0), [(sel("Q", s), rg("AB", 16 * l0 + s, 16 * m1, 16)) for s in range(16)])
-            d, n4 = rg(pd, 0, HL), rg(pn, 0, HL)
-            ts(H("md"), d, rg("thF"), None, A.max)
-            ts(n4, d, rg("thF"), rg("s4t"), A.is_lt, A.mult)
+            for mode, k in CHUNKS[h]:
+                m0, m1 = m1, m1 + k
+                cols, dcol = (16 * m0, 16 * m1), rg("D", 4096 * h + 16 * (m0 - p0), 4096 * h + 16 * (m1 - p0))
+                if mode == "v":
+                    g_tt(dcol, rg("hdS"), rg("PA", m0, m1), rg("hx", *cols), A.subtract)
+                    act(rg("AB", *cols), dcol, AF.Abs)
+                else:
+                    ps = rg(pq, 0, 16 * k)
+                    g_act(rg("V", *cols), rg("hdS"), rg("PA", m0, m1))
+                    mm(ps, [(rg("nI"), rg("hx", *cols)), (rg("ID"), rg("V", *cols))])
+                    act(rg("AB", *cols), ps, AF.Abs)
+                    act(dcol, ps, AF.Copy)
+                mms([(rg(pd, (m - p0) // 8, HL, 16), rg("AB", 16 * m, 16 * m + 128), dc) for m in range(m0, m1, 8)])
+            d, n4, fx = rg(pd, 0, HL), rg(pn, 0, HL), rg(pn, HL, 2 * HL)
+            tt(H("md"), d, rg("thT"), A.max)
+            tt(n4, d, rg("thT"), A.is_lt)
             ts(H("q4"), H("md"), 60, None, A.bitwise_and)
+            tt(n4, n4, rg("s4T"), A.mult)
             tt(n4, n4, H("q4"), A.add)
             X, rv = H("X"), rg(pq, 0, HL)
-            tt(X, n4, H("M0"), A.mult)
-            ts(H("fx"), n4, rg("s4"), 16.0, A.is_equal, A.mult)
-            act(H("gx"), H("fx"), AF.Identity, rg("sF"))
+            tt(X, n4, rg("M0"), A.mult)
+            ts(fx, n4, rg("s4"), None, A.is_equal)
             for k in range(5):
                 mm(rv, [(rg("BO"), X)])
                 E = H("E") if k < 4 else H("E5")
                 ts(E, rv, rg("s4"), None, A.is_equal)
                 if k < 4:
                     tt(X, n4, E, A.mult)
-            OL, pl = L("OL"), rg("pL", 16 + c0, 16 + c1)
-            tt(H("XF"), H("gx"), H("E5"), A.mult)
-            mm(pl, [(sel("Q", r), rg("XF", p0 + r, p1, 16)) for r in range(16)])
-            ts(L("bd"), pl, 16.0, 16.0, A.is_ge, A.mult)
-            tt(L("t2"), pl, rg("Lb", 0, c1 - c0), A.add)
-            tt(OL, L("t2"), L("bd"), A.subtract)
-            mu, hv, zB, am = rg(pq, HL, 2 * HL), rg(pd, HL, 2 * HL), rg(pq, 2 * HL, 3 * HL), rg(pn, 2 * HL, 3 * HL)
-            mm(mu, [(rg("B16"), H("XF")), (rg("BSn"), H("E5"))])
-            g_act(H("Dg"), rg("D", 16 * p0, 16 * p1), OL)
-            mm(hv, [(rg("ID2"), H(hb)), (rg("ID"), H("Dg"))])
-            act(H("Ba"), H("Dg"), AF.Abs)
-            mm(zB, [(rg("nB16"), H("XF")), (rg("BSp"), H("E5")), (rg("ID"), H("Ba"))])
-            act(H("bm"), zB, AF.Relu)
+            tt(H("XF"), fx, H("E5"), A.mult)
+            pl, ol = 64 + 64 * h, 32 * h
+            mm(rg("pL", pl, pl + 40), [(H("E5"), rg("RE")), (H("XF"), rg("RF"))])
+            tt(rg("OL", ol, ol + 32), rg("pL", pl, pl + 32), rg("LC%d" % h), A.add)
+            copy(L("bd"), rg("pL", pl + 32, pl + 40))
+            OL = lambda k: rg("OL", ol + 8 * k, ol + 8 * k + 8)
+            win = rg("D", 4096 * h, 4096 * h + 4096)
+            hv, zB = rg(pd, HL, 2 * HL), rg(pq, HL, 2 * HL)
+            g_act(H("Dg"), win, OL(0))
+            g_act(H("Bg"), win, OL(1), AF.Abs)
+            (g_copy if h else g_act)(H("hm"), rg(hb), OL(2))
+            mm(hv, [(rg("ID2"), H("hm")), (rg("ID"), H("Dg"))])
+            mm(zB, [(rg("ID"), H("Bg"))])
             ts(H("aI"), hv, 0.5, -0.25, A.mult, A.add)
-            tt(am, H("aI"), mu, A.mult)
-            tt(H("hn%d" % t), am, H("bm"), A.add)
-            for k, (s0, s1) in enumerate(SENDS):
-                if not p0 < s1 <= p1:
-                    continue
-                dst = T.cores[(rank + SHIFT) % N]
-                hn, nx = rg("hn%d" % t, s0, s1), rg("hb%d" % (t + 1), s0, s1)
-                def send(e, hn=hn, nx=nx, t=t, k=k, dst=dst):
-                    rid, pid = topo.addr(dst, core)
-                    e.remote_dma(ap(nx), ap(hn), T.sem["ar%d%d" % (t, k)], T.sem["sn%d%d" % (t, k)], pid, rid, topo.mask(core, dst))
-                    return []
-                ne = len(topo.engines(core, dst))
-                node("g", [("rem", 1)], [hn], [], send, sem="sn%d%d" % (t, k), count=ne, lat=[("net", 0.5)])
-                node("net", [], [], [nx], None, sem="ar%d%d" % (t, k), count=ne, lat=[("net", 1)], after=len(ops) - 1)
+            tt(H("hn%d" % t), zB, H("aI"), A.add)
+            dst = T.cores[(rank + SHIFT) % N]
+            hn, nx = rg("hn%d" % t, p0, p1), rg("hb%d" % (t + 1), p0, p1)
+            def send(e, hn=hn, nx=nx, t=t, h=h, dst=dst):
+                rid, pid = topo.addr(dst, core)
+                e.remote_dma(ap(nx), ap(hn), T.sem["ar%d%d" % (t, h)], T.sem["sn%d%d" % (t, h)], pid, rid, topo.mask(core, dst))
+                return []
+            ne = len(topo.engines(core, dst))
+            node("g", [("rem", 1)], [hn], [], send, sem="sn%d%d" % (t, h), count=ne, lat=[("net", 0.5)])
+            node("net", [], [], [nx], None, sem="ar%d%d" % (t, h), count=ne, lat=[("net", 1)], after=len(ops) - 1)
             nr, q0, q1 = (8, 0, 64) if h == 0 else (16, 64, 192)
             if h == 0:
                 g_tt(rg("val", q0, q1), rg("bd", 0, 8), rg("jh", 0, 4), rg("NE", q0, q1), A.add)
@@ -277,23 +321,25 @@ def build(T, rank, core, topo):
             scan(rg("sc", q0, q1), rg("RST", q0, q1), rg("val", q0, q1), 1000000.0, A.add, A.min)
             ts(L("ls"), rg("sc", q0 + nr - 1, q1, nr), 0.5, 16.0, A.is_le, A.mult)
             tt(L("kl"), L("bd"), L("ls"), A.max)
-            tt(L("kd"), L("kl"), L("dx"), A.mult)
-            tt(L("xs"), L("kd"), L("xf"), A.add)
-            tt(rg("pY", 256 + p0, 256 + p1), rg("pY", p0, p1), H("E5"), A.mult)
-            tt(H("col"), rg("pY", 256 + p0, 256 + p1), H("Ac"), A.add)
+            xs, col = L("xs%d" % t), H("col%d" % t)
+            tt(L("kd"), L("kl"), L("dmp"), A.mult)
+            tt(xs, L("kd"), L("xf"), A.max)
+            g_tt(H("t5"), rg("M0", 0, 16), OL(3), H("BA"), A.mult)
+            tt(col, rg("pY", 256 + p0, 256 + p1), H("t5"), A.add)
             if t < STEPS - 1:
-                scat(rg("D0"), L("xs"), H("KI"))
-                scat(rg("D1"), L("xs"), H("col"))
+                scat_add(rg("D0"), xs, rg("thT"), 1.0 / 8192, 0.0)
+                scat(rg("D1"), xs, col)
                 if t == STEPS - 2 and h == 1:
                     act(rg("YM", 0, W), rg("D0", 0, W), AF.Sign, 1.0, -1.0)
-            scat_add(rg("YO"), L("xs"), H("col"), 1536.0)
+            scat_add(rg("YO"), xs, col, 1536.0)
             if t == STEPS - 1:
-                scat(rg("YM"), L("xs"), H("K1"))
+                scat_add(rg("YM"), xs, rg("thT"), 1.0, 0.0)
     ctx["h"] = 2
     dma("sp", "syo", [rg("YO", 0, W)], [], lambda: T.yo[:], lambda: T.YO[:, 0:W], 3000)
     dma("act", "sym", [rg("YM", 0, W)], [], lambda: T.ym[:], lambda: T.YM[0:128:16, 0:W], 0)
-    for k, (s0, s1) in enumerate(SENDS):
-        dma("sp", "syh%d" % k, [rg("hb3", s0, s1)], [], lambda s0=s0, s1=s1: T.yh[:, s0:s1], lambda s0=s0, s1=s1: T.hb3[:, s0:s1], 200)
+    for h in range(2):
+        s0, s1 = HL * h, HL * h + HL
+        dma("sp", "syh%d" % h, [rg("hb3", s0, s1)], [], lambda s0=s0, s1=s1: T.yh[:, s0:s1], lambda s0=s0, s1=s1: T.hb3[:, s0:s1], 200)
     return ops
 
 

import numpy as np
from concourse.mybir import AluOpType as A, ActivationFunctionType as AF

N, P, W, R, STEPS, SHIFT = 8, 256, 1024, 3072, 3, 3
HL = 128
CHUNKS = [[("v", 64), ("a", 32), ("a", 32)], [("v", 64), ("v", 32), ("a", 32)]]
HXD = [2, 0]
HXG = [0, 6]
MAG = 12582912.0
INIT = 2000.0

COLF = ["sF", "s4", "s128", "thH", "thL", "taN", "s8F", "aF", "pb", "s8x", "F1", "F2", "F3"]
SCRATCH = {"cf": ("sbuf", [128, len(COLF)], "float32")}
for _n, _w in (("oc", W), ("D0", W + P), ("D1", W + P), ("YO", W + P), ("YM", W + P), ("ST", W), ("thT", HL), ("s4T", HL),
               ("pk0", 8), ("pS0", 16), ("pS", 16), ("LB0", 24), ("LB1", 24), ("LC0", 32), ("LC1", 32), ("dm0", 16), ("dm1", 16),
               ("dmp", 16), ("z16", 16), ("NE", P), ("RST", P), ("xf", 16), ("SF", P), ("a1", P), ("Rr", P), ("b1", P), ("B0", P),
               ("tw", P), ("BA", P), ("t5", P), ("col0", P), ("col1", P), ("col2", P),
               ("bd", 16), ("val", P), ("sc", P), ("ls", 16), ("kl", 16), ("kd", 16)):
    SCRATCH[_n] = ("sbuf", [128, _w], "float32")
for _n, _w in (("hdS", R), ("mkB", W), ("wS", 1), ("ones", 128), ("BO1", 128), ("BO", 128), ("G8", 128), ("Q", 144), ("WQ", 144),
               ("ID", 128), ("ID2", 128), ("nI", 128), ("TH", 128), ("TL", 128), ("TN", 128), ("RE", 40), ("RF", 40), ("M0", 128),
               ("hp", P), ("hx", 16 * P), ("D", 32 * P), ("AB", 16 * P), ("V", 16 * P), ("E", P), ("E5", P), ("X", P), ("XF", P),
               ("Dg", P), ("Bg", P), ("hm", P), ("hb0", 2 * P), ("hb1", 2 * P), ("hb2", 2 * P), ("hb3", P), ("hn0", P), ("hn1", P),
               ("hn2", P)):
    SCRATCH[_n] = ("sbuf", [128, _w], "bfloat16")
for _n, _w in (("ow", W), ("mkI", W), ("thI", 1), ("thX", 1), ("thY", 1), ("pI", 1), ("sI", 1), ("s8I", 1), ("aI1", 1), ("tauI", 1),
               ("mI", 128), ("mJ", 128), ("rI", P), ("uI", 16), ("uM", 16), ("u32", 16), ("pr", 16), ("rw", 16), ("vI", 16),
               ("vM", 16), ("v32", 16), ("vr", 16), ("vw", 16), ("md", P), ("q4", P), ("aI", P)):
    SCRATCH[_n] = ("sbuf", [128, _w], "int32")
for _n, _w in (("jl", 16), ("jh", 16), ("prm", 8), ("PA", P), ("xl", 16), ("xj", 16), ("OL", 64), ("xs0", 16), ("xs1", 16), ("xs2", 16)):
    SCRATCH[_n] = ("sbuf", [128, _w], "uint16")
PSUM = ["pd0", "pd1", "pn0", "pn1", "pr0", "pr1", "pL", "pY"]
for _n in PSUM:
    SCRATCH[_n] = ("psum", [128, 512], "float32")
QSEM = {"dve": "qv", "pe": "qt", "act": "qa", "g": "qg"}
DMAS = ["lh", "lw", "lt", "lm", "lo0", "lo1", "lr", "syo", "sym", "syh0", "syh1"]
SEMAPHORES = list(QSEM.values()) + DMAS + ["%s%d%d" % (k, t, h) for k in ("ar", "sn") for t in range(STEPS) for h in range(2)]
EST = {"c": 1.0, "g": 1.6, "s": 3.6, "op": 10.0, "wake": 80.0, "own": 40.0, "net": 2000.0, "rem": 600.0, "dma": 2200.0, "win": 100.0}
SC = [dict(), dict(c=.85, g=.9, s=1.5, wake=50), dict(c=1.2, g=2.4, s=6.5), dict(g=1.1, s=5.0, wake=150, own=80, rem=900, net=2500),
      dict(g=2.1, s=2.0, wake=30, own=20, rem=400, net=1500, dma=1800)]
TRIES = 3000
CACHE = {}


def build(T, rank, core, topo):
    ops, ctx = [], {"h": 0, "t": 0}

    def node(q, work, reads, writes, emit, **kw):
        nm = writes[0][0] if writes else kw.get("sem", "x")
        ops.append(dict(q=q, work=work, reads=reads, writes=writes, emit=emit, tag=nm + str(ctx["h"]), t=ctx["t"], **kw))

    def rg(name, a=0, b=None, st=1):
        if name in COLF:
            return ("cf", COLF.index(name), COLF.index(name) + 1, 1)
        return (name, a, SCRATCH[name][1][1] if b is None else b, st)

    def ap(r):
        n, a, b, st = r
        return T[n][:, a:b] if st == 1 else T[n][:, a:b:st]

    width = lambda r: (r[2] - r[1] + r[3] - 1) // r[3]
    ind = lambda win, off: ap(win).indirect(ap(off))
    isp = lambda r: r[0] in PSUM
    two = lambda r: SCRATCH[r[0]][2] in ("bfloat16", "uint16")
    cyc = lambda n, k=1.0: ("c", max(64, n * k))
    val = lambda s: ap(s) if isinstance(s, tuple) else s
    regs = lambda *s: [x for x in s if isinstance(x, tuple)]
    def copy(o, i):
        node("dve", [cyc(width(o), 0.5 if two(o) and two(i) else 1)], [i], [o], lambda e: [e.tensor_copy(ap(o), ap(i))])
    def tt(o, x, y, op):
        node("dve", [cyc(width(o), 1 if isp(x) or isp(y) else 2)], [x, y], [o], lambda e: [e.tensor_tensor(ap(o), ap(x), ap(y), op)])
    def ts(o, x, s1, s2, op0, op1=None):
        def emit(e):
            if op1 is None:
                return [e.tensor_scalar(ap(o), ap(x), val(s1), None, op0)]
            return [e.tensor_scalar(ap(o), ap(x), val(s1), val(s2), op0, op1)]
        node("dve", [cyc(width(o), 0.5 if two(o) and two(x) else 1)], [x] + regs(s1, s2), [o], emit)
    def fill(o, c):
        node("dve", [cyc(width(o), 0.5 if two(o) else 1)], [], [o], lambda e: [e.memset(ap(o), c)])
    def scan(o, x, y, init, op0, op1):
        node("dve", [cyc(width(o))], [x, y], [o], lambda e: [e.tensor_tensor_scan(ap(o), ap(x), ap(y), init, op0, op1)])
    def g_copy(o, win, off):
        node("dve", [("k", 55), ("g", width(o))], [win, off], [o], lambda e: [e.tensor_copy(ap(o), ind(win, off))])
    def g_tt(o, win, off, y, op):
        node("dve", [("k", 55), ("g", width(o))], [win, off, y], [o], lambda e: [e.tensor_tensor(ap(o), ind(win, off), ap(y), op)])
    def g_ts(o, win, off, s1, s2, op0, op1):
        node("dve", [("k", 55), ("g", width(o))], [win, off], [o], lambda e: [e.tensor_scalar(ap(o), ind(win, off), s1, s2, op0, op1)])
    def scat(win, off, i):
        node("dve", [("k", 55), ("s", width(i))], [i, off], [win], lambda e: [e.tensor_copy(ind(win, off), ap(i))])
    def scat_add(win, off, i, c, k=1.0):
        node("dve", [("k", 55), ("s", width(i))], [i, off], [win], lambda e: [e.tensor_scalar(ind(win, off), ap(i), k, c, A.mult, A.add)])
    def act(o, i, f, bias=0.0, scale=1.0):
        node("act", [cyc(width(o))], [i] + regs(bias, scale), [o], lambda e: [e.activation(ap(o), ap(i), f, bias=val(bias), scale=val(scale))])
    def g_act(o, win, off, f=AF.Copy):
        node("act", [("k", 70), ("g", width(o))], [win, off], [o], lambda e: [e.activation(ap(o), ind(win, off), f)])
    def mm(o, pairs):
        def emit(e):
            n = len(pairs)
            return [e.matmul(ap(o), ap(l), ap(r), j == 0, j == n - 1) for j, (l, r) in enumerate(pairs)]
        node("pe", [cyc(width(r)) for _, r in pairs], sorted(set([l for l, _ in pairs] + [r for _, r in pairs])), [o], emit)
    def mms(triples):
        node("pe", [cyc(width(r)) for _, _, r in triples], sorted(set([l for _, l, _ in triples] + [r for _, _, r in triples])),
             [o for o, _, _ in triples], lambda e: [e.matmul(ap(o), ap(l), ap(r), True, True) for o, l, r in triples])
    sel = lambda q, s: rg(q, 15 - s, 143 - s)
    def dma(q, sem, reads, writes, out, in_, ns):
        node(q, [("k", 60)], reads, writes, lambda e: [e.dma_start(out(), in_())], sem=sem, count=16, lat=[("dma", 1), ("k", ns)])

    dma("sp", "lm", [], [rg("mkI")], lambda: T.mkI[0:8, :], lambda: T.marks[:], 0)
    dma("act", "lw", [], [rg("wS")], lambda: T.wS[:], lambda: T.w[:], 0)
    dma("sp", "lo0", [], [rg("ow", 0, 512)], lambda: T.ow[:, 0:512], lambda: T.owner[:, 0:512], 1200)
    dma("act", "lh", [], [rg("hb0", 0, P)], lambda: T.hb0[:, 0:P], lambda: T.h0[:], 400)
    dma("sp", "lo1", [], [rg("ow", 512, W)], lambda: T.ow[:, 512:W], lambda: T.owner[:, 512:W], 2400)
    dma("act", "lt", [], [rg("thI")], lambda: T.thI[:], lambda: T.th[:], 1200)
    dma("sp", "lr", [], [rg("hdS")], lambda: T.hdS[:], lambda: T.hdr[:], 6000)

    fill(rg("ones"), 1.0)
    gn = lambda n, reads, o, f: node("g", [("k", 150), ("c", 2 * n)], reads, [o], lambda e: [f(e)])
    gn(128, [rg("ones")], rg("G8"), lambda e: e.affine_select(T.G8[0:8, :], T.ones[0:8, :], [[-1, 8], [0, 16]], A.is_equal, 0.0, 0, 1))
    gn(128, [rg("ones")], rg("BO1"), lambda e: e.affine_select(T.BO1[:], T.ones[:], [[-16, 8], [0, 16]], A.is_ge, 0.0, 0, 1))
    gn(128, [rg("BO1")], rg("BO"), lambda e: e.affine_select(T.BO[:], T.BO1[:], [[16, 8], [0, 16]], A.is_ge, 0.0, 15, -1))
    gn(1, [], rg("pI"), lambda e: e.iota(T.pI[:], [[1, 1]], 0, 1))
    fl = dict(allow_small_or_imprecise_dtypes=True)
    gn(16, [], rg("pS0"), lambda e: e.iota(T.pS0[:], [[0, 2], [2, 8]], 0, 0, **fl))
    gn(8, [], rg("pk0"), lambda e: e.iota(T.pk0[:], [[2, 8]], 0, 0, **fl))
    gn(128, [rg("ones")], rg("ID"), lambda e: e.affine_select(T.ID[:], T.ones[:], [[-1, 128]], A.is_equal, 0.0, 0, 1))
    gn(128, [], rg("mI"), lambda e: e.iota(T.mI[:], [[1, 128]], 128, -1))
    for h in range(2):
        lb = "LB%d" % h
        gn(16, [], rg(lb, 0, 16), lambda e, lb=lb: e.iota(T[lb][:, 0:16], [[-2048, 2], [16, 8]], 2048, 0, **fl))
        gn(8, [], rg(lb, 16, 24), lambda e, lb=lb, h=h: e.iota(T[lb][:, 16:24], [[16, 8]], 256 + 128 * h, 0, **fl))
    gn(16, [], rg("dm0"), lambda e: e.iota(T.dm0[:], [[16, 16]], W, 0, **fl))
    def zero(o):
        gn(width(o), [], o, lambda e: e.iota(ap(o), [[0, width(o)]], 0, 0, **fl))
    for k in range(2):
        zero(rg("hb%d" % k, P, 2 * P))
        zero(rg("D", 4096 * k + 2048, 4096 * k + 4096))
    zero(rg("hb2", P, 2 * P))
    gn(64, [], rg("rI", 0, 64), lambda e: e.iota(T.rI[:, 0:64], [[0, 8], [1, 8]], 0, 0))
    gn(128, [], rg("rI", 64, 192), lambda e: e.iota(T.rI[:, 64:192], [[0, 8], [1, 16]], 0, 0))

    fill(rg("Q"), 0.0)
    copy(rg("Q", 15, 143, 16), rg("BO", 0, 128, 16))
    ts(rg("WQ"), rg("Q"), rg("wS"), None, A.mult)
    ts(rg("sI"), rg("pI"), 15, None, A.bitwise_and)
    copy(rg("sF"), rg("sI"))
    ts(rg("s8I"), rg("sI"), 7, None, A.bitwise_and)
    copy(rg("s8F"), rg("s8I"))
    ts(rg("aI1"), rg("sI"), 3, None, A.arith_shift_right)
    copy(rg("aF"), rg("aI1"))
    ts(rg("s8x"), rg("s8F"), 16.0, None, A.mult)
    tt(rg("pb"), rg("s8x"), rg("aF"), A.add)
    ts(rg("prm"), rg("pk0"), rg("pb"), None, A.add)
    ts(rg("pS"), rg("pS0"), rg("aF"), None, A.add)
    node("dve", [cyc(1024)], [rg("mkI")], [rg("mkB")], lambda e: [e.tensor_copy(T.mkB[0:8, :], T.mkI[0:8, :])])
    for b in range(2):
        node("pe", [cyc(512)], [rg("G8"), rg("mkB", 512 * b, 512 * b + 512)], [rg("pd%d" % b)],
             lambda e, b=b: [e.matmul(T["pd%d" % b][:], T.G8[0:8, :], T.mkB[0:8, 512 * b:512 * b + 512], True, True)])
    B = lambda n, b: rg(n, 512 * b, 512 * b + 512)
    for b in range(2):
        act(B("D0", b), rg("pd%d" % b), AF.Identity, 1.0, 1.0 / 8192 - 1.0)
        ts(B("oc", b), B("ow", b), -1536.0, None, A.add)
        tt(B("D1", b), rg("pd%d" % b), B("oc", b), A.mult)
    ts(rg("s4"), rg("sF"), 4.0, None, A.mult)
    ts(rg("s128"), rg("sF"), 128.0, None, A.mult)
    ts(rg("mJ"), rg("mI"), 15, None, A.bitwise_and)
    ts(rg("M0"), rg("mJ"), 0.0, None, A.is_equal)
    ts(rg("thX"), rg("thI"), 8128, None, A.bitwise_and)
    ts(rg("thY"), rg("thI"), 63, None, A.bitwise_and)
    ts(rg("tauI"), rg("thI"), 60, None, A.bitwise_and)
    copy(rg("thH"), rg("thX"))
    copy(rg("thL"), rg("thY"))
    ts(rg("taN"), rg("tauI"), -1.0, None, A.mult)
    ts(rg("TH"), rg("BO"), rg("thH"), None, A.mult)
    ts(rg("TL"), rg("BO"), rg("thL"), None, A.mult)
    ts(rg("TN"), rg("BO"), rg("taN"), None, A.mult)
    mm(rg("pn0", 0, HL), [(rg("M0"), rg("TH")), (rg("M0"), rg("TL"))])
    mm(rg("pn0", HL, 2 * HL), [(rg("M0"), rg("TN"))])
    copy(rg("thT"), rg("pn0", 0, HL))
    ts(rg("s4T"), rg("pn0", HL, 2 * HL), rg("s4"), None, A.add)
    ts(rg("ID2"), rg("ID"), 2.0, None, A.mult)
    ts(rg("nI"), rg("ID"), -1.0, None, A.mult)
    dc = rg("BO", 0, 128, 16)
    fill(rg("RE"), 0.0)
    fill(rg("RF"), 0.0)
    for k in (0, 1, 3):
        ts(rg("RE", 8 * k, 8 * k + 8), dc, rg("sF"), None, A.mult)
    for k, c in ((0, -2048.0), (1, 2048.0), (2, -256.0), (4, 16.0)):
        ts(rg("RF", 8 * k, 8 * k + 8), dc, c, None, A.mult)
    for h in range(2):
        ts(rg("LC%d" % h, 0, 16), rg("LB%d" % h, 0, 16), rg("s128"), None, A.add)
        ts(rg("LC%d" % h, 16, 24), rg("LB%d" % h, 16, 24), rg("sF"), None, A.add)
        fill(rg("LC%d" % h, 24, 32), 0.0)
    ts(rg("dm1"), rg("dm0"), rg("sF"), None, A.add)
    ts(rg("dmp"), rg("dm1"), 1.0 / 16, None, A.mult)
    fill(rg("z16"), 0.0)
    ts(rg("jl"), rg("z16"), rg("sF"), None, A.add)
    ts(rg("jh"), rg("z16"), rg("s8F"), None, A.add)
    fill(rg("NE"), 10000.0)
    ts(rg("RST", 0, 192), rg("rI", 0, 192), 0.0, 1000000.0, A.is_equal, A.mult)
    act(rg("YO", 0, W), rg("oc"), AF.Identity, 1536.0)

    for t in range(STEPS):
        ctx["t"] = t
        hb = "hb%d" % t
        for h in range(2):
            ctx["h"] = h
            p0, p1 = HL * h, HL * h + HL
            g_act(rg("hp", p0, p1), rg(hb, p0, p1), rg("prm"))
            for s in range(16):
                o, i = rg("hx", 16 * p0 + s, 16 * p1, 16), rg("hp", p0, p1)
                if s < HXD[h]:
                    copy(o, i)
                elif s >= 16 - HXG[h]:
                    gn(HL, [i], o, lambda e, o=o, i=i: e.affine_select(ap(o), ap(i), [[0, HL]], A.is_ge, 0.0, 0, 0))
                else:
                    act(o, i, AF.Copy)
            mm(rg("pL", 8 * h, 8 * h + 8), [(sel("WQ", q), rg(hb, p0 + 16 * (q % 8) + q // 8, p0 + 16 * (q % 8) + 16, 2)) for q in range(16)])
        ctx["h"] = 0
        copy(rg("uI"), rg("pL", 0, 16))
        ts(rg("uM"), rg("uI"), 4095, None, A.bitwise_and)
        ts(rg("u32"), rg("uM"), 32.0, None, A.add)
        tt(rg("pr"), rg("uM"), rg("u32"), A.mult)
        ts(rg("rw"), rg("pr"), 5, 1008, A.arith_shift_right, A.bitwise_and)
        tt(rg("xl"), rg("rw"), rg("pS"), A.add)
        mm(rg("pL", 16, 32), [(sel("WQ", r), rg(hb, r, P, 16)) for r in range(16)])
        copy(rg("vI"), rg("pL", 16, 32))
        ts(rg("vM"), rg("vI"), 4095, None, A.bitwise_and)
        ts(rg("v32"), rg("vM"), 32.0, None, A.add)
        tt(rg("vr"), rg("vM"), rg("v32"), A.mult)
        ts(rg("vw"), rg("vr"), 5, 1008, A.arith_shift_right, A.bitwise_and)
        ts(rg("xj"), rg("vw"), rg("sF"), None, A.add)
        ts(rg("xf"), rg("vw"), rg("sF"), None, A.add)
        scan(rg("ST"), rg("D0", 0, W), rg("D1", 0, W), INIT, A.mult, A.add)
        for h in range(2):
            ctx["h"] = h
            g_ts(rg("PA", HL * h, HL * h + HL), rg("ST"), rg("xl", 8 * h, 8 * h + 8), MAG + 1536.0, MAG, A.add, A.subtract)
        for h in range(2):
            ctx["h"] = h
            base = lambda c: c * 8 if c < 8 else 64 + (c - 8) * 16
            def emit_ne(e, cs=range(max(1, 8 * h), 8 * h + 8), base=base):
                return [e.activation(T.NE[:, base(c):base(c) + c], T.xf[:, 0:c], AF.Abs, bias=T.xf[:, c:c + 1], scale=-1.0) for c in cs]
            node("act", [cyc(16)] * 8, [rg("xf")], [rg("NE", 0, 64) if h == 0 else rg("NE", 64, 192)], emit_ne)
        ctx["h"] = 0
        pA, pB = rg("pY", 256, 512), rg("pY", 0, 256)
        g_act(rg("SF"), rg("ST"), rg("xj"))
        ts(rg("F1"), rg("ST", W - 1, W), MAG, MAG, A.add, A.subtract)
        ts(rg("F2"), rg("F1"), -1.0, INIT, A.mult, A.add)
        ts(rg("F3"), rg("F2"), -1999.0, None, A.mult)
        act(rg("a1"), rg("SF"), AF.Identity, MAG)
        act(pA, rg("a1"), AF.Identity, -MAG)
        tt(rg("Rr"), rg("SF"), pA, A.subtract)
        act(rg("b1"), rg("Rr"), AF.Identity, MAG, 8192.0)
        act(rg("B0"), rg("b1"), AF.Identity, -MAG)
        act(rg("tw"), rg("B0"), AF.Relu, rg("F3"), rg("F2"))
        tt(pB, rg("B0"), pA, A.subtract)
        tt(rg("BA"), pB, rg("tw"), A.subtract)
        for h in range(2):
            ctx["h"] = h
            p0, p1, c0, c1 = HL * h, HL * h + HL, 8 * h, 8 * h + 8
            H = lambda name: rg(name, p0, p1)
            L = lambda name: rg(name, c0, c1)
            pd, pn, pq = "pd%d" % h, "pn%d" % h, "pr%d" % h
            m1 = p0
            for mode, k in CHUNKS[h]:
                m0, m1 = m1, m1 + k
                cols, dcol = (16 * m0, 16 * m1), rg("D", 4096 * h + 16 * (m0 - p0), 4096 * h + 16 * (m1 - p0))
                if mode == "v":
                    g_tt(dcol, rg("hdS"), rg("PA", m0, m1), rg("hx", *cols), A.subtract)
                    act(rg("AB", *cols), dcol, AF.Abs)
                else:
                    ps = rg(pq, 0, 16 * k)
                    g_act(rg("V", *cols), rg("hdS"), rg("PA", m0, m1))
                    mm(ps, [(rg("nI"), rg("hx", *cols)), (rg("ID"), rg("V", *cols))])
                    act(rg("AB", *cols), ps, AF.Abs)
                    act(dcol, ps, AF.Copy)
                mms([(rg(pd, (m - p0) // 8, HL, 16), rg("AB", 16 * m, 16 * m + 128), dc) for m in range(m0, m1, 8)])
            d, n4, fx = rg(pd, 0, HL), rg(pn, 0, HL), rg(pn, HL, 2 * HL)
            tt(H("md"), d, rg("thT"), A.max)
            tt(n4, d, rg("thT"), A.is_lt)
            ts(H("q4"), H("md"), 60, None, A.bitwise_and)
            tt(n4, n4, rg("s4T"), A.mult)
            tt(n4, n4, H("q4"), A.add)
            X, rv = H("X"), rg(pq, 0, HL)
            tt(X, n4, rg("M0"), A.mult)
            ts(fx, n4, rg("s4"), None, A.is_equal)
            for k in range(5):
                mm(rv, [(rg("BO"), X)])
                E = H("E") if k < 4 else H("E5")
                ts(E, rv, rg("s4"), None, A.is_equal)
                if k < 4:
                    tt(X, n4, E, A.mult)
            tt(H("XF"), fx, H("E5"), A.mult)
            pl, ol = 64 + 64 * h, 32 * h
            mm(rg("pL", pl, pl + 40), [(H("E5"), rg("RE")), (H("XF"), rg("RF"))])
            tt(rg("OL", ol, ol + 32), rg("pL", pl, pl + 32), rg("LC%d" % h), A.add)
            copy(L("bd"), rg("pL", pl + 32, pl + 40))
            OL = lambda k: rg("OL", ol + 8 * k, ol + 8 * k + 8)
            win = rg("D", 4096 * h, 4096 * h + 4096)
            hv, zB = rg(pd, HL, 2 * HL), rg(pq, HL, 2 * HL)
            g_act(H("Dg"), win, OL(0))
            g_act(H("Bg"), win, OL(1), AF.Abs)
            (g_copy if h else g_act)(H("hm"), rg(hb), OL(2))
            mm(hv, [(rg("ID2"), H("hm")), (rg("ID"), H("Dg"))])
            mm(zB, [(rg("ID"), H("Bg"))])
            ts(H("aI"), hv, 0.5, -0.25, A.mult, A.add)
            tt(H("hn%d" % t), zB, H("aI"), A.add)
            dst = T.cores[(rank + SHIFT) % N]
            hn, nx = rg("hn%d" % t, p0, p1), rg("hb%d" % (t + 1), p0, p1)
            def send(e, hn=hn, nx=nx, t=t, h=h, dst=dst):
                rid, pid = topo.addr(dst, core)
                e.remote_dma(ap(nx), ap(hn), T.sem["ar%d%d" % (t, h)], T.sem["sn%d%d" % (t, h)], pid, rid, topo.mask(core, dst))
                return []
            ne = len(topo.engines(core, dst))
            node("g", [("rem", 1)], [hn], [], send, sem="sn%d%d" % (t, h), count=ne, lat=[("net", 0.5)])
            node("net", [], [], [nx], None, sem="ar%d%d" % (t, h), count=ne, lat=[("net", 1)], after=len(ops) - 1)
            nr, q0, q1 = (8, 0, 64) if h == 0 else (16, 64, 192)
            if h == 0:
                g_tt(rg("val", q0, q1), rg("bd", 0, 8), rg("jh", 0, 4), rg("NE", q0, q1), A.add)
            else:
                g_tt(rg("val", q0, q1), rg("bd"), rg("jl", 0, 8), rg("NE", q0, q1), A.add)
            scan(rg("sc", q0, q1), rg("RST", q0, q1), rg("val", q0, q1), 1000000.0, A.add, A.min)
            ts(L("ls"), rg("sc", q0 + nr - 1, q1, nr), 0.5, 16.0, A.is_le, A.mult)
            tt(L("kl"), L("bd"), L("ls"), A.max)
            xs, col = L("xs%d" % t), H("col%d" % t)
            tt(L("kd"), L("kl"), L("dmp"), A.mult)
            tt(xs, L("kd"), L("xf"), A.max)
            g_tt(H("t5"), rg("M0", 0, 16), OL(3), H("BA"), A.mult)
            tt(col, rg("pY", 256 + p0, 256 + p1), H("t5"), A.add)
            if t < STEPS - 1:
                scat_add(rg("D0"), xs, rg("thT"), 1.0 / 8192, 0.0)
                scat(rg("D1"), xs, col)
                if t == STEPS - 2 and h == 1:
                    act(rg("YM", 0, W), rg("D0", 0, W), AF.Sign, 1.0, -1.0)
            scat_add(rg("YO"), xs, col, 1536.0)
            if t == STEPS - 1:
                scat_add(rg("YM"), xs, rg("thT"), 1.0, 0.0)
    ctx["h"] = 2
    dma("sp", "syo", [rg("YO", 0, W)], [], lambda: T.yo[:], lambda: T.YO[:, 0:W], 3000)
    dma("act", "sym", [rg("YM", 0, W)], [], lambda: T.ym[:], lambda: T.YM[0:128:16, 0:W], 0)
    for h in range(2):
        s0, s1 = HL * h, HL * h + HL
        dma("sp", "syh%d" % h, [rg("hb3", s0, s1)], [], lambda s0=s0, s1=s1: T.yh[:, s0:s1], lambda s0=s0, s1=s1: T.hb3[:, s0:s1], 200)
    return ops


def meet(a, b):
    if a[1] >= b[2] or b[1] >= a[2]:
        return False
    if a[3] == b[3] and a[3] > 1:
        return (a[1] - b[1]) % a[3] == 0
    return True


def depend(ops):
    hist, deps = {}, []
    for i, o in enumerate(ops):
        d = {}
        for w, regs in ((0, o["reads"]), (1, o["writes"])):
            for r in regs:
                for (j, pw, pr) in hist.get(r[0], []):
                    same = ops[j]["q"] == o["q"] and o["q"] != "net"
                    bank = r[0] in PSUM and not same
                    if bank or ((w or pw) and meet(r, pr)):
                        d[j] = d.get(j, False) or not same or bool(pw)
        if "after" in o:
            d[o["after"]] = True
        d.pop(i, None)
        deps.append(d)
        for w, regs in ((0, o["reads"]), (1, o["writes"])):
            for r in regs:
                lst = hist.setdefault(r[0], [])
                if w and r[0] not in PSUM and r[3] == 1:
                    lst[:] = [x for x in lst if not (r[1] <= x[2][1] and x[2][2] <= r[2])]
                lst.append((i, w, r))
    return deps


def price(work, est):
    return sum(n if k == "k" else n * est[k] + (est["op"] if k == "c" else 0.0) for k, n in work)


def schedule(ops, deps, est, bias):
    n = len(ops)
    cost = [price(o["work"], est) for o in ops]
    lat = [price(o.get("lat", []), est) for o in ops]
    succ = [[] for _ in range(n)]
    for i in range(n):
        for j in deps[i]:
            succ[j].append(i)
    prio = [0.0] * n
    for i in range(n - 1, -1, -1):
        prio[i] = cost[i] + lat[i] + max([prio[k] + (est["wake"] if ops[k]["q"] != ops[i]["q"] else est["own"]) for k in succ[i]] + [0.0])
    rank = [prio[i] + bias.get(ops[i]["tag"], 0.0) for i in range(n)]
    left = [len(deps[i]) for i in range(n)]
    free, fin, order, begin = {}, [0.0] * n, [], [0.0] * n
    ready = {}

    def enter(i):
        q = ops[i]["q"]
        s = 0.0
        for j, hard in deps[i].items():
            if ops[j]["q"] != q:
                s = max(s, fin[j] + est["wake"])
            elif hard:
                s = max(s, fin[j] + est["own"])
        begin[i] = s
        ready.setdefault(q, []).append(i)
    for i in range(n):
        if left[i] == 0:
            enter(i)
    while True:
        bq, bs = None, 1e18
        for q, lst in ready.items():
            if lst:
                s = max(free.get(q, 0.0), min(begin[i] for i in lst))
                if s < bs:
                    bq, bs = q, s
        if bq is None:
            break
        c = [i for i in ready[bq] if begin[i] <= bs + est["win"]]
        i = max(c, key=lambda k: rank[k] - max(0.0, begin[k] - bs))
        ready[bq].remove(i)
        order.append(i)
        end = max(free.get(bq, 0.0), begin[i]) + cost[i]
        if bq != "net":
            free[bq] = end
        fin[i] = end + lat[i]
        for k in succ[i]:
            left[k] -= 1
            if left[k] == 0:
                enter(k)
    return order


def tune(ops, deps):
    n = len(ops)
    q = [o["q"] for o in ops]
    pars = []
    for sc in SC:
        e = dict(EST)
        e.update(sc)
        pars.append((e, [price(o["work"], e) for o in ops], [price(o.get("lat", []), e) for o in ops]))
    dl = [[(j, q[j] == q[i]) for j, hard in deps[i].items() if hard or q[j] != q[i] or q[i] == "net"] for i in range(n)]

    def span(order, e, cost, lat):
        fin, free = [0.0] * n, {}
        for i in order:
            f = free.get(q[i], 0.0) if q[i] != "net" else 0.0
            t = f
            for j, same in dl[i]:
                x = fin[j]
                if x > f - 1e-9 or same:
                    t = max(t, x + (e["own"] if same else e["wake"]))
            free[q[i]] = t + cost[i]
            fin[i] = t + cost[i] + lat[i]
        return max(fin)
    best, order = {}, schedule(ops, deps, EST, {})
    base = [span(order, *p) for p in pars]
    score = float(len(pars))
    tags = sorted(set(o["tag"] for o in ops if o["q"] in QSEM))
    rnd = np.random.RandomState(0)
    for _ in range(TRIES):
        b = dict(best)
        for _ in range([1, 1, 2, 3, 5][int(rnd.randint(5))]):
            k = tags[int(rnd.randint(len(tags)))]
            if rnd.rand() < 0.2:
                b.pop(k, None)
            else:
                b[k] = float(round(b.get(k, 0.0) + 3000.0 * rnd.randn()))
        o = schedule(ops, deps, EST, b)
        v = sum(span(o, *p) / x for p, x in zip(pars, base))
        if v < score - 1e-7:
            best, order, score = b, o, v
    return order


def rank_program(g, core, T, topo):
    rank = T.rank_of(core)
    if rank is None:
        return
    ops = build(T, rank, core, topo)
    if "order" not in CACHE:
        CACHE["deps"] = depend(ops)
        CACHE["order"] = tune(ops, CACHE["deps"])
    deps, order = CACHE["deps"], CACHE["order"]
    eng = {"dve": g.vector, "pe": g.tensor, "act": g.scalar, "g": g, "sp": g.sync}
    total, known, done = {}, {q: {} for q in eng}, {}
    for i in order:
        o = ops[i]
        q = o["q"]
        if q == "net":
            total[o["sem"]] = o["count"]
            done[i] = (o["sem"], o["count"], {})
            continue
        need, clocks = {}, {}
        for j, hard in deps[i].items():
            if ops[j]["q"] == q and not hard:
                continue
            s, v, ck = done[j]
            if v > need.get(s, 0):
                need[s], clocks[s] = v, ck
        kn = known[q]
        todo = [(s, v) for s, v in need.items() if kn.get(s, 0) < v]
        for s, v in todo:
            if not any(s2 != s and clocks[s2].get(s, 0) >= v for s2, _ in todo):
                eng[q].wait_ge(T.sem[s], v)
        for s, v in todo:
            kn[s] = max(kn.get(s, 0), v)
            for s3, v3 in clocks[s].items():
                kn[s3] = max(kn.get(s3, 0), v3)
        ins = o["emit"](eng[q])
        if "sem" in o:
            for x in ins:
                x.then_inc(T.sem[o["sem"]], o["count"])
            total[o["sem"]] = o["count"]
            done[i] = (o["sem"], o["count"], dict(kn))
        else:
            s = QSEM[q]
            for x in ins:
                x.then_inc(T.sem[s], 1)
            total[s] = total.get(s, 0) + len(ins)
            done[i] = (s, total[s], dict(kn))
    for s, v in total.items():
        if known["g"].get(s, 0) < v:
            g.wait_ge(T.sem[s], v)
